import numpy as np
import ml_dtypes


def mxq(x, axis, fmt="e4m3"):
    dtype, down = {"e4m3": (ml_dtypes.float8_e4m3fn, 7), "e5m2": (ml_dtypes.float8_e5m2, 14)}[fmt]
    v = np.moveaxis(np.asarray(x, np.float32).astype(ml_dtypes.bfloat16).astype(np.float64), axis, -1)
    blocks = v.reshape(v.shape[:-1] + (-1, 32))
    amax = np.abs(blocks).max(-1, keepdims=True)
    byte = np.maximum(np.where(amax > 0, np.frexp(amax)[1] - 1 + 127, 0) - down, 1)
    scale = np.exp2(byte - 127.0)
    codes = (blocks / scale).astype(np.float32).astype(dtype).astype(np.float64)
    return np.moveaxis((codes * scale).reshape(v.shape), -1, axis)


WIDE = False


def mx_kscale(k):
    if not WIDE:
        return np.ones(k)
    levels = np.array([10, -10, 5, -5, 0])
    if k % 512:
        return np.exp2(np.random.permutation(np.resize(levels, k // 32))).repeat(32)
    a = np.empty((k // 512, 16))
    for p in range(k // 512):
        a[p, :8] = np.random.permutation(np.resize(levels, 8))
        for g in range(8):
            far = levels[np.abs(levels - a[p, g]) >= 10]
            a[p, g + 8] = far[np.random.randint(len(far))]
    return np.exp2(a.ravel()).repeat(32)


BF16 = ml_dtypes.bfloat16


def bf(x):
    return np.asarray(x, np.float32).astype(BF16)


def f64(x):
    return np.asarray(x).astype(np.float64)


B, N, D, E = 2, 1024, 512, 512

EPS = 1e-6


def rms_normalize(z):
    mean_sq = np.mean(z * z, axis=-1, keepdims=True)
    return z / np.sqrt(mean_sq + EPS)


def draw0():
    s, t = mx_kscale(N), mx_kscale(D)
    return {"q": bf(np.random.standard_normal((B, N, D)) / t[None, None, :]),
            "k": bf(np.random.standard_normal((B, N, D)) * s[None, :, None] * t[None, None, :]),
            "v": bf(np.random.standard_normal((B, N, E)) / np.sqrt(N) / s[None, :, None]),
            "gc": bf(np.random.standard_normal(D)),
            "gt": bf(np.random.standard_normal(N))}


def core(q, k, v, gc, gt):
    q, k, v, gc, gt = f64(q), f64(k), f64(v), f64(gc), f64(gt)
    n = q.shape[1]

    qa = np.maximum(q, 0.0) * gc[None, None, :]
    ka = np.maximum(k, 0.0) * gt[None, :, None]

    th = np.pi * np.arange(n) / (2.0 * n)
    c = np.cos(th)[None, :, None]
    s = np.sin(th)[None, :, None]

    qc = qa * c
    qs = qa * s
    kc = ka * c
    ks = ka * s

    vq = mxq(v, 1, "e4m3")
    mc = mxq(kc, 1, "e4m3").transpose(0, 2, 1) @ vq
    ms = mxq(ks, 1, "e4m3").transpose(0, 2, 1) @ vq

    z = (mxq(qc, 2, "e4m3") @ mxq(mc, 1, "e4m3")) + (mxq(qs, 2, "e4m3") @ mxq(ms, 1, "e4m3"))

    return rms_normalize(z)


def e4m3fn_bytes(y):
    return np.clip(np.asarray(y, np.float64), -448.0, 448.0).astype(np.float32).astype(ml_dtypes.float8_e4m3fn).view(np.uint8)


def e4m3fn_values(b):
    return np.asarray(b, np.uint8).view(ml_dtypes.float8_e4m3fn).astype(np.float64)


def setup_inputs():
    d = draw0()
    x0 = np.asarray(d['v']).astype(np.float64)
    s = (np.max(np.abs(x0), axis=(0, 2), keepdims=True) / 448.0).astype(np.float32)
    out = {}
    for k, v in d.items():
        if k == 'v':
            out['v_bytes'] = e4m3fn_bytes(x0 / s.astype(np.float64))
            out['v_scale'] = s
        else:
            out[k] = v
    return out


def reference(q, k, v_bytes, v_scale, gc, gt):
    return core(q, k, e4m3fn_values(v_bytes) * v_scale.astype(np.float64), gc, gt)

@@ -1,0 +1,300 @@
+import math
+from contextlib import ExitStack
+
+import concourse.mybir as mybir
+from concourse.masks import make_identity
+
+B, N, D, E = 2, 1024, 512, 512
+FLOPS = 2 * 4 * 2 * N * D * E
+EPS = 1e-6
+
+P = 128
+T = 4
+G = N // (P * T)
+F32 = mybir.dt.float32
+BF16 = mybir.dt.bfloat16
+U32 = mybir.dt.uint32
+U8 = mybir.dt.uint8
+FP8 = mybir.dt.float8_e4m3fn
+FP8X4 = mybir.dt.float8_e4m3fn_x4
+ACT = mybir.ActivationFunctionType
+ALU = mybir.AluOpType
+
+
+def tile_cosformernormlinearattention_kernel(tc, q, k, v_bytes, v_scale, gc, gt, out):
+    nc = tc.nc
+    with ExitStack() as ctx:
+        const = ctx.enter_context(tc.tile_pool(name="const", bufs=1))
+        loads = ctx.enter_context(tc.tile_pool(name="loads", bufs=1))
+        work = ctx.enter_context(tc.tile_pool(name="work", bufs=4))
+        keep = ctx.enter_context(tc.tile_pool(name="keep", bufs=1))
+        outp = ctx.enter_context(tc.tile_pool(name="outp", bufs=3))
+        psum = ctx.enter_context(tc.psum_pool(name="psum", bufs=2))
+
+        gt_col = const.tile([P, G, T], BF16, name="gt_col")
+        gc_col = const.tile([P, T], BF16, name="gc_col")
+        vs_col = const.tile([P, G, T], F32, name="vs_col")
+        nc.scalar.dma_start(out=gt_col[:], in_=gt.rearrange("(g p t) -> p g t", p=P, t=T))
+        nc.scalar.dma_start(out=vs_col[:], in_=v_scale.rearrange("o (g p t) x -> p (o g) (t x)", p=P, t=T))
+        nc.scalar.dma_start(out=gc_col[:], in_=gc.rearrange("(p t) -> p t", t=T))
+
+        k_raw, v_raw, q_raw = {}, {}, {}
+
+        def load_kv(b, g):
+            kt = loads.tile([P, T, D], BF16, name="k_raw%d%d" % (b, g))
+            nc.sync.dma_start(out=kt[:], in_=k[b].rearrange("(g p t) d -> g p t d", p=P, t=T)[g])
+            vt = loads.tile([P, T, E], U8, name="v_raw%d%d" % (b, g))
+            nc.sync.dma_start(out=vt[:], in_=v_bytes[b].rearrange("(g p t) d -> g p t d", p=P, t=T)[g])
+            k_raw[b, g], v_raw[b, g] = kt, vt
+
+        def load_q(b, w):
+            qt = loads.tile([P, 2, D], BF16, name="q_raw%d%d" % (b, w))
+            nc.sync.dma_start(out=qt[:], in_=q[b].rearrange("(w i r) d -> w r i d", i=2, r=P)[w])
+            q_raw[b, w] = qt
+
+        for b in range(B):
+            for g in range(G):
+                load_kv(b, g)
+            for w in range(4):
+                load_q(b, w)
+
+        idx_col = const.tile([P, 2, G, T], F32, name="idx_col")
+        nc.gpsimd.iota(idx_col[:, 0], pattern=[[-512, G], [-1, T]], base=N, channel_multiplier=-T,
+                       allow_small_or_imprecise_dtypes=True)
+        nc.gpsimd.iota(idx_col[:, 1], pattern=[[512, G], [1, T]], base=0, channel_multiplier=T,
+                       allow_small_or_imprecise_dtypes=True)
+        idx_row = const.tile([P, N + 1], F32, name="idx_row")
+        nc.gpsimd.iota(idx_row[:], pattern=[[1, N + 1]], base=0, channel_multiplier=0,
+                       allow_small_or_imprecise_dtypes=True)
+        ident = const.tile([P, P], BF16, name="ident")
+        make_identity(nc, ident[:])
+
+        step = math.pi / (2 * N)
+        trig_col = const.tile([P, 2, G, T], F32, name="trig_col")
+        nc.scalar.activation(out=trig_col[:], in_=idx_col[:], func=ACT.Sin, scale=step)
+        sin_row = const.tile([P, N + 1], F32, name="sin_row")
+        nc.scalar.activation(out=sin_row[:], in_=idx_row[:], func=ACT.Sin, scale=step)
+
+        kscale = const.tile([P, 2, G, T], F32, name="kscale")
+        for h in range(2):
+            nc.vector.tensor_tensor(out=kscale[:, h], in0=trig_col[:, h], in1=gt_col[:], op=ALU.mult)
+        gate = const.tile([P, N + 1, T], F32, name="gate")
+
+        def gate_chunk(i):
+            lo = i * 256
+            hi = lo + 256 + (1 if i == 3 else 0)
+            nc.vector.tensor_tensor(
+                out=gate[:, lo:hi, :],
+                in0=sin_row[:, lo:hi].unsqueeze(2).to_broadcast([P, hi - lo, T]),
+                in1=gc_col[:].unsqueeze(1).to_broadcast([P, hi - lo, T]),
+                op=ALU.mult)
+
+        planes, inter, codes, scales = {}, {}, {}, {}
+
+        def scale_unit(b, kind, g):
+            pl = work.tile([P, T, D], BF16, name="planes")
+            for t in range(T):
+                if kind == 2:
+                    nc.vector.tensor_scalar(out=pl[:, t], in0=v_raw[b, g][:, t].bitcast(FP8),
+                                            scalar1=vs_col[:, g, t:t + 1], scalar2=None, op0=ALU.mult)
+                else:
+                    nc.vector.tensor_scalar(out=pl[:, t], in0=k_raw[b, g][:, t], scalar1=0.0,
+                                            scalar2=kscale[:, kind, g, t:t + 1], op0=ALU.max, op1=ALU.mult)
+            planes[b, kind, g] = pl
+
+        def interleave(b, kind, g, eng):
+            it = work.tile([P, D * T], BF16, name="inter", align_bytes=64)
+            pl = planes[b, kind, g]
+            if kind == 2:
+                dst = it[:].rearrange("p (c i t) -> p c t i", i=4, t=T)
+                src = pl[:].rearrange("p t (c i) -> p c t i", i=4)
+            else:
+                dst = it[:].rearrange("p (s m t) -> p m t s", s=4, t=T)
+                src = pl[:].rearrange("p t (m s) -> p m t s", s=4)
+            if eng == "V":
+                nc.vector.tensor_copy(out=dst, in_=src)
+            else:
+                nc.scalar.copy(out=dst, in_=src)
+            inter[b, kind, g] = it
+
+        def quant_unit(b, kind, g):
+            cd = keep.tile([P, D], U32, name="codes%d%d%d" % (b, kind, g), align_bytes=64)
+            sc = keep.tile([P, D], U8, name="scales%d%d%d" % (b, kind, g), align_bytes=64)
+            nc.vector.quantize_mx(out=cd[:].bitcast(FP8X4), scales=sc[:], in_=inter[b, kind, g][:])
+            codes[b, kind, g], scales[b, kind, g] = cd, sc
+
+        m_inter, m_codes, m_scales = {}, {}, {}
+
+        def m_block(b, h, eb, eng):
+            if eb == 0:
+                m_inter[b, h] = work.tile([P, E, T], BF16, name="m_inter", align_bytes=64)
+            bank = psum.tile([P, T, P], F32, name="m_bank", bufs=2)
+            es = slice(eb * P, (eb + 1) * P)
+            for s in range(T):
+                for g in range(G):
+                    nc.tensor.matmul_mx(
+                        out=bank[:, s],
+                        lhsT=codes[b, h, g][:, s * P:(s + 1) * P].bitcast(FP8X4),
+                        lhsT_scale=scales[b, h, g][:, s * P:(s + 1) * P],
+                        rhs=codes[b, 2, g][:, es].bitcast(FP8X4),
+                        rhs_scale=scales[b, 2, g][:, es],
+                        start=(g == 0), stop=(g == G - 1))
+            dst = m_inter[b, h][:, es, :]
+            src = bank[:].rearrange("p s e -> p e s")
+            if eng == "V":
+                nc.vector.tensor_copy(out=dst, in_=src)
+            else:
+                nc.scalar.copy(out=dst, in_=src)
+
+        def m_quant(b, h):
+            cd = keep.tile([P, E], U32, name="mcodes%d%d" % (b, h), align_bytes=64)
+            sc = keep.tile([P, E], U8, name="mscales%d%d" % (b, h), align_bytes=64)
+            nc.vector.quantize_mx(out=cd[:].bitcast(FP8X4), scales=sc[:],
+                                  in_=m_inter[b, h][:].rearrange("p e s -> p (e s)"))
+            m_codes[b, h], m_scales[b, h] = cd, sc
+
+        q_turned, q_inter, q_codes, q_scales = {}, {}, {}, {}
+
+        def q_turn(b, w):
+            bank = psum.tile([P, T, 2, P], BF16, name="t_bank", bufs=2)
+            for i in range(2):
+                for t in range(T):
+                    nc.tensor.transpose(bank[:, t, i], q_raw[b, w][:, i, t::T], ident[:])
+            q_turned[b, w] = bank
+
+        def q_gate(b, w):
+            qi = work.tile([P, 2, 256, T], BF16, name="q_inter", align_bytes=64)
+            src = q_turned[b, w][:].rearrange("p t i r -> p (i r) t")
+            n0 = w * 256
+            for h in range(2):
+                if h == 0:
+                    tab = gate[:, N - n0:N - n0 - 256:-1, :]
+                else:
+                    tab = gate[:, n0:n0 + 256, :]
+                nc.vector.scalar_tensor_tensor(out=qi[:, h], in0=src, scalar=0.0, in1=tab,
+                                               op0=ALU.max, op1=ALU.mult)
+            q_inter[b, w] = qi
+
+        def q_quant(b, w):
+            cd = work.tile([P, 2, 256], U32, name="q_codes", align_bytes=64)
+            sc = work.tile([P, 2, 256], U8, name="q_scales", align_bytes=64)
+            nc.vector.quantize_mx(out=cd[:].rearrange("p h n -> p (h n)").bitcast(FP8X4),
+                                  scales=sc[:].rearrange("p h n -> p (h n)"),
+                                  in_=q_inter[b, w][:].rearrange("p h n t -> p (h n t)"))
+            q_codes[b, w], q_scales[b, w] = cd, sc
+
+        def z_pair(b, w, engs):
+            ss = outp.tile([P, 2], F32, name="ss")
+            rstd = outp.tile([P, 2], F32, name="rstd")
+            res = outp.tile([P, 2, E], F32, name="res")
+            banks = []
+            for i in range(2):
+                bank = psum.tile([P, E], F32, name="z_bank", bufs=4)
+                cols = slice(i * P, (i + 1) * P)
+                for h in range(2):
+                    nc.tensor.matmul_mx(
+                        out=bank[:],
+                        lhsT=q_codes[b, w][:, h, cols].bitcast(FP8X4),
+                        lhsT_scale=q_scales[b, w][:, h, cols],
+                        rhs=m_codes[b, h][:].bitcast(FP8X4),
+                        rhs_scale=m_scales[b, h][:],
+                        start=(h == 0), stop=(h == 1))
+                banks.append(bank)
+            for i in range(2):
+                junk = outp.tile([P, E], BF16, name="junk")
+                nc.scalar.activation(out=junk[:], in_=banks[i][:], func=ACT.Square, accum_out=ss[:, i:i + 1])
+            nc.scalar.activation(out=rstd[:], in_=ss[:], func=ACT.Abs_reciprocal_sqrt, scale=1.0 / E, bias=EPS)
+            for i in range(2):
+                if engs[i] == "V":
+                    nc.vector.tensor_scalar(out=res[:, i], in0=banks[i][:], scalar1=rstd[:, i:i + 1],
+                                            scalar2=None, op0=ALU.mult)
+                else:
+                    nc.scalar.activation(out=res[:, i], in_=banks[i][:], func=ACT.Copy, scale=rstd[:, i:i + 1])
+            nc.sync.dma_start(out=out[b].rearrange("(w i r) e -> w r i e", i=2, r=P)[w], in_=res[:])
+
+        KC, KS, V = 0, 1, 2
+
+        gate_chunk(0)
+        scale_unit(0, V, 0)
+        scale_unit(0, KC, 0)
+        interleave(0, V, 0, "S")
+        scale_unit(0, V, 1)
+        interleave(0, KC, 0, "V")
+        scale_unit(0, KC, 1)
+        gate_chunk(1)
+        quant_unit(0, KC, 0)
+        interleave(0, V, 1, "S")
+        interleave(0, KC, 1, "V")
+        scale_unit(0, KS, 0)
+        quant_unit(0, V, 0)
+        interleave(0, KS, 0, "S")
+        gate_chunk(2)
+        quant_unit(0, KC, 1)
+        scale_unit(0, KS, 1)
+        q_turn(0, 0)
+        q_turn(0, 1)
+        gate_chunk(3)
+        interleave(0, KS, 1, "V")
+        quant_unit(0, V, 1)
+        for eb in range(4):
+            m_block(0, 0, eb, "S")
+        quant_unit(0, KS, 0)
+        quant_unit(0, KS, 1)
+        scale_unit(1, V, 0)
+        q_gate(0, 0)
+        for eb in range(4):
+            m_block(0, 1, eb, "S")
+        interleave(1, V, 0, "S")
+        scale_unit(1, V, 1)
+        q_gate(0, 1)
+        q_quant(0, 0)
+        m_quant(0, 0)
+        q_turn(0, 2)
+        interleave(1, V, 1, "S")
+        q_turn(0, 3)
+        scale_unit(1, KC, 0)
+        q_gate(0, 2)
+        q_quant(0, 1)
+        m_quant(0, 1)
+        z_pair(0, 0, "SS")
+        scale_unit(1, KC, 1)
+        interleave(1, KC, 0, "S")
+        q_gate(0, 3)
+        q_quant(0, 2)
+        z_pair(0, 1, "SS")
+        scale_unit(1, KS, 0)
+        q_quant(0, 3)
+        interleave(1, KC, 1, "V")
+        quant_unit(1, V, 0)
+        quant_unit(1, V, 1)
+        z_pair(0, 2, "SS")
+        scale_unit(1, KS, 1)
+        quant_unit(1, KC, 0)
+        interleave(1, KS, 0, "V")
+        quant_unit(1, KC, 1)
+        for eb in range(4):
+            m_block(1, 0, eb, "S")
+        interleave(1, KS, 1, "V")
+        quant_unit(1, KS, 0)
+        z_pair(0, 3, "SS")
+        q_turn(1, 0)
+        q_turn(1, 1)
+        quant_unit(1, KS, 1)
+        q_gate(1, 0)
+        for eb in range(4):
+            m_block(1, 1, eb, "S")
+        m_quant(1, 0)
+        q_gate(1, 1)
+        q_quant(1, 0)
+        q_turn(1, 2)
+        q_turn(1, 3)
+        m_quant(1, 1)
+        q_gate(1, 2)
+        q_quant(1, 1)
+        z_pair(1, 0, "SS")
+        q_gate(1, 3)
+        q_quant(1, 2)
+        z_pair(1, 1, "SS")
+        q_quant(1, 3)
+        z_pair(1, 2, "SV")
+        z_pair(1, 3, "SV")

@@ -30,6 +30,7 @@ def tile_cosformernormlinearattention_kernel(tc, q, k, v_bytes, v_scale, gc, gt,
         keep = ctx.enter_context(tc.tile_pool(name="keep", bufs=1))
         outp = ctx.enter_context(tc.tile_pool(name="outp", bufs=3))
         psum = ctx.enter_context(tc.psum_pool(name="psum", bufs=2))
+        ctx.enter_context(tc.manual_schedule())
 
         gt_col = const.tile([P, G, T], BF16, name="gt_col")
         gc_col = const.tile([P, T], BF16, name="gc_col")
@@ -41,10 +42,10 @@ def tile_cosformernormlinearattention_kernel(tc, q, k, v_bytes, v_scale, gc, gt,
         k_raw, v_raw, q_raw = {}, {}, {}
 
         def load_kv(b, g):
-            kt = loads.tile([P, T, D], BF16, name="k_raw%d%d" % (b, g))
-            nc.sync.dma_start(out=kt[:], in_=k[b].rearrange("(g p t) d -> g p t d", p=P, t=T)[g])
             vt = loads.tile([P, T, E], U8, name="v_raw%d%d" % (b, g))
             nc.sync.dma_start(out=vt[:], in_=v_bytes[b].rearrange("(g p t) d -> g p t d", p=P, t=T)[g])
+            kt = loads.tile([P, T, D], BF16, name="k_raw%d%d" % (b, g))
+            nc.sync.dma_start(out=kt[:], in_=k[b].rearrange("(g p t) d -> g p t d", p=P, t=T)[g])
             k_raw[b, g], v_raw[b, g] = kt, vt
 
         def load_q(b, w):
@@ -92,7 +93,7 @@ def tile_cosformernormlinearattention_kernel(tc, q, k, v_bytes, v_scale, gc, gt,
         planes, inter, codes, scales = {}, {}, {}, {}
 
         def scale_unit(b, kind, g):
-            pl = work.tile([P, T, D], BF16, name="planes")
+            pl = work.tile([P, T, D], BF16, name="planes", bufs=8)
             for t in range(T):
                 if kind == 2:
                     nc.vector.tensor_scalar(out=pl[:, t], in0=v_raw[b, g][:, t].bitcast(FP8),
@@ -102,10 +103,15 @@ def tile_cosformernormlinearattention_kernel(tc, q, k, v_bytes, v_scale, gc, gt,
                                             scalar2=kscale[:, kind, g, t:t + 1], op0=ALU.max, op1=ALU.mult)
             planes[b, kind, g] = pl
 
-        def interleave(b, kind, g, eng):
-            it = work.tile([P, D * T], BF16, name="inter", align_bytes=64)
-            pl = planes[b, kind, g]
-            if kind == 2:
+        def inter_tile(u):
+            if u not in inter:
+                inter[u] = work.tile([P, D * T], BF16, name="inter", align_bytes=64, bufs=6)
+            return inter[u]
+
+        def interleave(u, eng):
+            it = inter_tile(u)
+            pl = planes[u]
+            if u[1] == 2:
                 dst = it[:].rearrange("p (c i t) -> p c t i", i=4, t=T)
                 src = pl[:].rearrange("p t (c i) -> p c t i", i=4)
             else:
@@ -115,19 +121,34 @@ def tile_cosformernormlinearattention_kernel(tc, q, k, v_bytes, v_scale, gc, gt,
                 nc.vector.tensor_copy(out=dst, in_=src)
             else:
                 nc.scalar.copy(out=dst, in_=src)
-            inter[b, kind, g] = it
 
-        def quant_unit(b, kind, g):
-            cd = keep.tile([P, D], U32, name="codes%d%d%d" % (b, kind, g), align_bytes=64)
-            sc = keep.tile([P, D], U8, name="scales%d%d%d" % (b, kind, g), align_bytes=64)
-            nc.vector.quantize_mx(out=cd[:].bitcast(FP8X4), scales=sc[:], in_=inter[b, kind, g][:])
-            codes[b, kind, g], scales[b, kind, g] = cd, sc
+        i_bank = {}
 
-        m_inter, m_codes, m_scales = {}, {}, {}
+        def turn_planes(u, a):
+            bank = psum.tile([P, 2, D], BF16, name="zi_bank", bufs=4)
+            for j in range(2):
+                s = 2 * a + j
+                if u[1] == 2:
+                    src = planes[u][:].rearrange("p t (s m) -> p s m t", s=4)[:, s]
+                else:
+                    src = planes[u][:].rearrange("p t (m s) -> p s m t", s=4)[:, s]
+                nc.tensor.matmul(bank[:, j], lhsT=ident[:], rhs=src, start=True, stop=True)
+            i_bank[u, a] = bank
 
-        def m_block(b, h, eb, eng):
-            if eb == 0:
-                m_inter[b, h] = work.tile([P, E, T], BF16, name="m_inter", align_bytes=64)
+        def copy_planes(u, a, eng):
+            it = inter_tile(u)
+            (nc.vector.tensor_copy if eng == "V" else nc.scalar.copy)(
+                out=it[:, a * 1024:(a + 1) * 1024], in_=i_bank[u, a][:].rearrange("p j d -> p (j d)"))
+
+        def quant_unit(u):
+            cd = keep.tile([P, D], U32, name="codes%d%d%d" % u, align_bytes=64)
+            sc = keep.tile([P, D], U8, name="scales%d%d%d" % u, align_bytes=64)
+            nc.vector.quantize_mx(out=cd[:].bitcast(FP8X4), scales=sc[:], in_=inter[u][:])
+            codes[u], scales[u] = cd, sc
+
+        m_inter, m_codes, m_scales, m_bank = {}, {}, {}, {}
+
+        def m_mult(b, h, eb):
             bank = psum.tile([P, T, P], F32, name="m_bank", bufs=2)
             es = slice(eb * P, (eb + 1) * P)
             for s in range(T):
@@ -139,12 +160,14 @@ def tile_cosformernormlinearattention_kernel(tc, q, k, v_bytes, v_scale, gc, gt,
                         rhs=codes[b, 2, g][:, es].bitcast(FP8X4),
                         rhs_scale=scales[b, 2, g][:, es],
                         start=(g == 0), stop=(g == G - 1))
-            dst = m_inter[b, h][:, es, :]
-            src = bank[:].rearrange("p s e -> p e s")
-            if eng == "V":
-                nc.vector.tensor_copy(out=dst, in_=src)
-            else:
-                nc.scalar.copy(out=dst, in_=src)
+            m_bank[b, h, eb] = bank
+
+        def m_copy(b, h, eb, eng):
+            if (b, h) not in m_inter:
+                m_inter[b, h] = keep.tile([P, E, T], BF16, name="m_inter%d%d" % (b, h), align_bytes=64)
+            dst = m_inter[b, h][:, eb * P:(eb + 1) * P, :]
+            src = m_bank[b, h, eb][:].rearrange("p s e -> p e s")
+            (nc.vector.tensor_copy if eng == "V" else nc.scalar.copy)(out=dst, in_=src)
 
         def m_quant(b, h):
             cd = keep.tile([P, E], U32, name="mcodes%d%d" % (b, h), align_bytes=64)
@@ -162,18 +185,17 @@ def tile_cosformernormlinearattention_kernel(tc, q, k, v_bytes, v_scale, gc, gt,
                     nc.tensor.transpose(bank[:, t, i], q_raw[b, w][:, i, t::T], ident[:])
             q_turned[b, w] = bank
 
-        def q_gate(b, w):
-            qi = work.tile([P, 2, 256, T], BF16, name="q_inter", align_bytes=64)
+        def q_gate(b, w, h):
+            if (b, w) not in q_inter:
+                q_inter[b, w] = work.tile([P, 2, 256, T], BF16, name="q_inter", align_bytes=64)
             src = q_turned[b, w][:].rearrange("p t i r -> p (i r) t")
             n0 = w * 256
-            for h in range(2):
-                if h == 0:
-                    tab = gate[:, N - n0:N - n0 - 256:-1, :]
-                else:
-                    tab = gate[:, n0:n0 + 256, :]
-                nc.vector.scalar_tensor_tensor(out=qi[:, h], in0=src, scalar=0.0, in1=tab,
-                                               op0=ALU.max, op1=ALU.mult)
-            q_inter[b, w] = qi
+            if h == 0:
+                tab = gate[:, N - n0:N - n0 - 256:-1, :]
+            else:
+                tab = gate[:, n0:n0 + 256, :]
+            nc.vector.scalar_tensor_tensor(out=q_inter[b, w][:, h], in0=src, scalar=0.0, in1=tab,
+                                           op0=ALU.max, op1=ALU.mult)
 
         def q_quant(b, w):
             cd = work.tile([P, 2, 256], U32, name="q_codes", align_bytes=64)
@@ -183,118 +205,226 @@ def tile_cosformernormlinearattention_kernel(tc, q, k, v_bytes, v_scale, gc, gt,
                                   in_=q_inter[b, w][:].rearrange("p h n t -> p (h n t)"))
             q_codes[b, w], q_scales[b, w] = cd, sc
 
-        def z_pair(b, w, engs):
-            ss = outp.tile([P, 2], F32, name="ss")
-            rstd = outp.tile([P, 2], F32, name="rstd")
-            res = outp.tile([P, 2, E], F32, name="res")
-            banks = []
-            for i in range(2):
-                bank = psum.tile([P, E], F32, name="z_bank", bufs=4)
-                cols = slice(i * P, (i + 1) * P)
-                for h in range(2):
-                    nc.tensor.matmul_mx(
-                        out=bank[:],
-                        lhsT=q_codes[b, w][:, h, cols].bitcast(FP8X4),
-                        lhsT_scale=q_scales[b, w][:, h, cols],
-                        rhs=m_codes[b, h][:].bitcast(FP8X4),
-                        rhs_scale=m_scales[b, h][:],
-                        start=(h == 0), stop=(h == 1))
-                banks.append(bank)
-            for i in range(2):
-                junk = outp.tile([P, E], BF16, name="junk")
-                nc.scalar.activation(out=junk[:], in_=banks[i][:], func=ACT.Square, accum_out=ss[:, i:i + 1])
-            nc.scalar.activation(out=rstd[:], in_=ss[:], func=ACT.Abs_reciprocal_sqrt, scale=1.0 / E, bias=EPS)
-            for i in range(2):
-                if engs[i] == "V":
-                    nc.vector.tensor_scalar(out=res[:, i], in0=banks[i][:], scalar1=rstd[:, i:i + 1],
-                                            scalar2=None, op0=ALU.mult)
-                else:
-                    nc.scalar.activation(out=res[:, i], in_=banks[i][:], func=ACT.Copy, scale=rstd[:, i:i + 1])
-            nc.sync.dma_start(out=out[b].rearrange("(w i r) e -> w r i e", i=2, r=P)[w], in_=res[:])
+        z_bank, z_ss, z_rstd, z_res = {}, {}, {}, {}
 
-        KC, KS, V = 0, 1, 2
+        def z_mult(b, w, i):
+            bank = psum.tile([P, E], F32, name="zi_bank", bufs=4)
+            cols = slice(i * P, (i + 1) * P)
+            for h in range(2):
+                nc.tensor.matmul_mx(
+                    out=bank[:],
+                    lhsT=q_codes[b, w][:, h, cols].bitcast(FP8X4),
+                    lhsT_scale=q_scales[b, w][:, h, cols],
+                    rhs=m_codes[b, h][:].bitcast(FP8X4),
+                    rhs_scale=m_scales[b, h][:],
+                    start=(h == 0), stop=(h == 1))
+            z_bank[b, w, i] = bank
 
-        gate_chunk(0)
-        scale_unit(0, V, 0)
-        scale_unit(0, KC, 0)
-        interleave(0, V, 0, "S")
-        scale_unit(0, V, 1)
-        interleave(0, KC, 0, "V")
-        scale_unit(0, KC, 1)
-        gate_chunk(1)
-        quant_unit(0, KC, 0)
-        interleave(0, V, 1, "S")
-        interleave(0, KC, 1, "V")
-        scale_unit(0, KS, 0)
-        quant_unit(0, V, 0)
-        interleave(0, KS, 0, "S")
+        def z_square(b, w, i):
+            junk = outp.tile([P, E], BF16, name="junk")
+            ss = outp.tile([P, 1], F32, name="ss")
+            nc.scalar.activation(out=junk[:], in_=z_bank[b, w, i][:], func=ACT.Square, accum_out=ss[:])
+            z_ss[b, w, i] = ss
+
+        def z_rsqrt(b, w, i):
+            rstd = outp.tile([P, 1], F32, name="rstd")
+            nc.scalar.activation(out=rstd[:], in_=z_ss[b, w, i][:], func=ACT.Abs_reciprocal_sqrt,
+                                 scale=1.0 / E, bias=EPS)
+            z_rstd[b, w, i] = rstd
+
+        def z_scale(b, w, i, eng):
+            res = outp.tile([P, E], F32, name="res", bufs=6)
+            if eng == "V":
+                nc.vector.tensor_scalar(out=res[:], in0=z_bank[b, w, i][:], scalar1=z_rstd[b, w, i][:],
+                                        scalar2=None, op0=ALU.mult)
+            else:
+                nc.scalar.activation(out=res[:], in_=z_bank[b, w, i][:], func=ACT.Copy, scale=z_rstd[b, w, i][:])
+            nc.sync.dma_start(out=out[b].rearrange("(w i r) e -> w i r e", i=2, r=P)[w, i], in_=res[:])
+
+        scale_unit(0, 2, 0)
+        scale_unit(0, 1, 0)
+        turn_planes((0, 2, 0), 0)
+        scale_unit(0, 0, 0)
+        interleave((0, 1, 0), "S")
         gate_chunk(2)
-        quant_unit(0, KC, 1)
-        scale_unit(0, KS, 1)
+        turn_planes((0, 0, 0), 0)
+        scale_unit(0, 1, 1)
         q_turn(0, 0)
-        q_turn(0, 1)
-        gate_chunk(3)
-        interleave(0, KS, 1, "V")
-        quant_unit(0, V, 1)
-        for eb in range(4):
-            m_block(0, 0, eb, "S")
-        quant_unit(0, KS, 0)
-        quant_unit(0, KS, 1)
-        scale_unit(1, V, 0)
-        q_gate(0, 0)
-        for eb in range(4):
-            m_block(0, 1, eb, "S")
-        interleave(1, V, 0, "S")
-        scale_unit(1, V, 1)
-        q_gate(0, 1)
-        q_quant(0, 0)
-        m_quant(0, 0)
+        scale_unit(0, 2, 1)
+        interleave((0, 1, 1), "S")
         q_turn(0, 2)
-        interleave(1, V, 1, "S")
-        q_turn(0, 3)
-        scale_unit(1, KC, 0)
-        q_gate(0, 2)
-        q_quant(0, 1)
-        m_quant(0, 1)
-        z_pair(0, 0, "SS")
-        scale_unit(1, KC, 1)
-        interleave(1, KC, 0, "S")
-        q_gate(0, 3)
-        q_quant(0, 2)
-        z_pair(0, 1, "SS")
-        scale_unit(1, KS, 0)
-        q_quant(0, 3)
-        interleave(1, KC, 1, "V")
-        quant_unit(1, V, 0)
-        quant_unit(1, V, 1)
-        z_pair(0, 2, "SS")
-        scale_unit(1, KS, 1)
-        quant_unit(1, KC, 0)
-        interleave(1, KS, 0, "V")
-        quant_unit(1, KC, 1)
-        for eb in range(4):
-            m_block(1, 0, eb, "S")
-        interleave(1, KS, 1, "V")
-        quant_unit(1, KS, 0)
-        z_pair(0, 3, "SS")
-        q_turn(1, 0)
-        q_turn(1, 1)
-        quant_unit(1, KS, 1)
-        q_gate(1, 0)
-        for eb in range(4):
-            m_block(1, 1, eb, "S")
-        m_quant(1, 0)
-        q_gate(1, 1)
-        q_quant(1, 0)
-        q_turn(1, 2)
+        quant_unit((0, 1, 0))
+        scale_unit(1, 2, 0)
+        turn_planes((0, 0, 0), 1)
+        scale_unit(1, 1, 0)
+        copy_planes((0, 2, 0), 0, "S")
+        turn_planes((0, 2, 0), 1)
+        scale_unit(1, 2, 1)
+        copy_planes((0, 0, 0), 0, "S")
+        interleave((0, 2, 1), "S")
+        turn_planes((1, 1, 0), 1)
+        scale_unit(1, 1, 1)
+        gate_chunk(3)
+        turn_planes((1, 1, 1), 0)
+        scale_unit(0, 0, 1)
+        copy_planes((0, 2, 0), 1, "S")
+        quant_unit((0, 2, 1))
+        copy_planes((1, 1, 1), 0, "S")
+        turn_planes((1, 1, 0), 0)
+        quant_unit((0, 2, 0))
+        interleave((0, 0, 1), "S")
+        quant_unit((0, 1, 1))
+        turn_planes((1, 2, 1), 0)
+        q_gate(0, 0, 0)
+        m_mult(0, 1, 3)
+        gate_chunk(0)
+        copy_planes((1, 1, 0), 0, "S")
+        m_mult(0, 1, 1)
+        quant_unit((0, 0, 1))
+        m_copy(0, 1, 3, "S")
+        q_gate(0, 0, 1)
+        copy_planes((1, 1, 0), 1, "S")
+        turn_planes((1, 2, 1), 1)
+        m_copy(0, 1, 1, "S")
+        quant_unit((1, 1, 0))
+        copy_planes((1, 2, 1), 0, "S")
+        m_mult(0, 1, 0)
+        copy_planes((0, 0, 0), 1, "S")
+        q_quant(0, 0)
         q_turn(1, 3)
-        m_quant(1, 1)
-        q_gate(1, 2)
-        q_quant(1, 1)
-        z_pair(1, 0, "SS")
-        q_gate(1, 3)
-        q_quant(1, 2)
-        z_pair(1, 1, "SS")
+        copy_planes((1, 2, 1), 1, "S")
+        scale_unit(1, 0, 1)
+        m_copy(0, 1, 0, "S")
+        quant_unit((0, 0, 0))
+        m_mult(0, 1, 2)
+        interleave((1, 2, 0), "S")
+        quant_unit((1, 2, 1))
+        interleave((1, 0, 1), "V")
+        m_mult(0, 0, 1)
+        turn_planes((1, 1, 1), 1)
+        m_copy(0, 1, 2, "V")
+        m_copy(0, 0, 1, "S")
+        quant_unit((1, 0, 1))
+        m_mult(0, 0, 3)
+        copy_planes((1, 1, 1), 1, "S")
+        quant_unit((1, 2, 0))
+        m_mult(0, 0, 0)
+        m_quant(0, 1)
+        m_copy(0, 0, 3, "S")
+        quant_unit((1, 1, 1))
+        m_mult(0, 0, 2)
+        m_copy(0, 0, 0, "S")
+        gate_chunk(1)
+        m_mult(1, 1, 1)
+        m_copy(0, 0, 2, "S")
+        scale_unit(1, 0, 0)
+        q_gate(0, 2, 0)
+        m_mult(1, 1, 3)
+        m_copy(1, 1, 1, "S")
+        interleave((1, 0, 0), "S")
+        m_mult(1, 1, 2)
+        m_quant(0, 0)
+        q_gate(0, 2, 1)
+        z_mult(0, 0, 1)
+        z_mult(0, 0, 0)
+        q_gate(1, 3, 0)
+        m_copy(1, 1, 3, "S")
+        q_turn(0, 3)
+        quant_unit((1, 0, 0))
+        m_copy(1, 1, 2, "S")
+        z_square(0, 0, 1)
+        q_gate(1, 3, 1)
+        m_mult(1, 0, 2)
+        z_square(0, 0, 0)
+        q_gate(0, 3, 0)
+        m_mult(1, 0, 0)
+        z_rsqrt(0, 0, 1)
+        m_copy(1, 0, 2, "S")
+        z_rsqrt(0, 0, 0)
+        q_turn(0, 1)
+        z_scale(0, 0, 1, "S")
+        q_quant(0, 2)
+        z_scale(0, 0, 0, "S")
+        q_gate(0, 3, 1)
+        m_copy(1, 0, 0, "S")
+        z_mult(0, 2, 1)
+        q_gate(0, 1, 0)
+        m_mult(1, 0, 1)
+        z_square(0, 2, 1)
+        m_mult(1, 0, 3)
+        q_quant(0, 3)
+        m_copy(1, 0, 1, "S")
+        q_gate(0, 1, 1)
+        z_rsqrt(0, 2, 1)
+        q_turn(1, 2)
+        m_copy(1, 0, 3, "S")
         q_quant(1, 3)
-        z_pair(1, 2, "SV")
-        z_pair(1, 3, "SV")
+        z_scale(0, 2, 1, "S")
+        m_mult(1, 1, 0)
+        m_quant(1, 0)
+        q_gate(1, 2, 0)
+        z_mult(0, 3, 1)
+        z_mult(0, 2, 0)
+        q_quant(0, 1)
+        z_square(0, 3, 1)
+        q_gate(1, 2, 1)
+        z_mult(0, 3, 0)
+        z_square(0, 2, 0)
+        z_mult(0, 1, 0)
+        z_rsqrt(0, 3, 1)
+        z_square(0, 3, 0)
+        m_copy(1, 1, 0, "V")
+        q_turn(1, 0)
+        q_quant(1, 2)
+        z_scale(0, 3, 1, "S")
+        m_quant(1, 1)
+        z_rsqrt(0, 3, 0)
+        z_square(0, 1, 0)
+        z_mult(0, 1, 1)
+        z_scale(0, 3, 0, "S")
+        q_gate(1, 0, 0)
+        z_rsqrt(0, 1, 0)
+        q_turn(1, 1)
+        z_rsqrt(0, 2, 0)
+        z_square(0, 1, 1)
+        z_scale(0, 2, 0, "V")
+        z_scale(0, 1, 0, "S")
+        q_gate(1, 0, 1)
+        z_mult(1, 3, 1)
+        z_rsqrt(0, 1, 1)
+        z_scale(0, 1, 1, "S")
+        z_mult(1, 2, 1)
+        q_gate(1, 1, 0)
+        z_square(1, 3, 1)
+        z_mult(1, 2, 0)
+        z_square(1, 2, 1)
+        q_quant(1, 0)
+        z_mult(1, 3, 0)
+        z_rsqrt(1, 3, 1)
+        z_rsqrt(1, 2, 1)
+        z_scale(1, 3, 1, "V")
+        z_square(1, 2, 0)
+        q_gate(1, 1, 1)
+        z_scale(1, 2, 1, "S")
+        z_mult(1, 0, 1)
+        z_rsqrt(1, 2, 0)
+        z_square(1, 3, 0)
+        z_mult(1, 0, 0)
+        z_scale(1, 2, 0, "S")
+        q_quant(1, 1)
+        z_rsqrt(1, 3, 0)
+        z_square(1, 0, 1)
+        z_mult(1, 1, 0)
+        z_scale(1, 3, 0, "V")
+        z_square(1, 0, 0)
+        z_mult(1, 1, 1)
+        z_rsqrt(1, 0, 1)
+        z_square(1, 1, 0)
+        z_scale(1, 0, 1, "V")
+        z_rsqrt(1, 0, 0)
+        z_square(1, 1, 1)
+        z_scale(1, 0, 0, "V")
+        z_rsqrt(1, 1, 0)
+        z_rsqrt(1, 1, 1)
+        z_scale(1, 1, 0, "V")
+        z_scale(1, 1, 1, "S")

@@ -92,16 +92,26 @@ def tile_cosformernormlinearattention_kernel(tc, q, k, v_bytes, v_scale, gc, gt,
 
         planes, inter, codes, scales = {}, {}, {}, {}
 
-        def scale_unit(b, kind, g):
-            pl = work.tile([P, T, D], BF16, name="planes", bufs=8)
+        def planes_tile(u):
+            if u not in planes:
+                planes[u] = work.tile([P, T, D], BF16, name="planes", bufs=8)
+            return planes[u]
+
+        def scale_k(b, kind, g):
+            pl = planes_tile((b, kind, g))
             for t in range(T):
-                if kind == 2:
-                    nc.vector.tensor_scalar(out=pl[:, t], in0=v_raw[b, g][:, t].bitcast(FP8),
-                                            scalar1=vs_col[:, g, t:t + 1], scalar2=None, op0=ALU.mult)
+                nc.vector.tensor_scalar(out=pl[:, t], in0=k_raw[b, g][:, t], scalar1=0.0,
+                                        scalar2=kscale[:, kind, g, t:t + 1], op0=ALU.max, op1=ALU.mult)
+
+        def scale_v(b, g, half, eng):
+            pl = planes_tile((b, 2, g))
+            for t in (2 * half, 2 * half + 1):
+                src = v_raw[b, g][:, t].bitcast(FP8)
+                factor = vs_col[:, g, t:t + 1]
+                if eng == "V":
+                    nc.vector.tensor_scalar(out=pl[:, t], in0=src, scalar1=factor, scalar2=None, op0=ALU.mult)
                 else:
-                    nc.vector.tensor_scalar(out=pl[:, t], in0=k_raw[b, g][:, t], scalar1=0.0,
-                                            scalar2=kscale[:, kind, g, t:t + 1], op0=ALU.max, op1=ALU.mult)
-            planes[b, kind, g] = pl
+                    nc.scalar.activation(out=pl[:, t], in_=src, func=ACT.Copy, scale=factor)
 
         def inter_tile(u):
             if u not in inter:
@@ -187,34 +197,33 @@ def tile_cosformernormlinearattention_kernel(tc, q, k, v_bytes, v_scale, gc, gt,
 
         def q_gate(b, w, h):
             if (b, w) not in q_inter:
-                q_inter[b, w] = work.tile([P, 2, 256, T], BF16, name="q_inter", align_bytes=64)
-            src = q_turned[b, w][:].rearrange("p t i r -> p (i r) t")
+                q_inter[b, w] = work.tile([P, 2, 2, P, T], BF16, name="q_inter", align_bytes=64)
+                q_codes[b, w] = work.tile([P, 2, 2, P], U32, name="q_codes", align_bytes=64)
+                q_scales[b, w] = work.tile([P, 2, 2, P], U8, name="q_scales", align_bytes=64)
+            src = q_turned[b, w][:].rearrange("p t i r -> p i r t")
             n0 = w * 256
             if h == 0:
                 tab = gate[:, N - n0:N - n0 - 256:-1, :]
             else:
                 tab = gate[:, n0:n0 + 256, :]
-            nc.vector.scalar_tensor_tensor(out=q_inter[b, w][:, h], in0=src, scalar=0.0, in1=tab,
+            nc.vector.scalar_tensor_tensor(out=q_inter[b, w][:, :, h], in0=src, scalar=0.0,
+                                           in1=tab.rearrange("p (i r) t -> p i r t", i=2),
                                            op0=ALU.max, op1=ALU.mult)
 
-        def q_quant(b, w):
-            cd = work.tile([P, 2, 256], U32, name="q_codes", align_bytes=64)
-            sc = work.tile([P, 2, 256], U8, name="q_scales", align_bytes=64)
-            nc.vector.quantize_mx(out=cd[:].rearrange("p h n -> p (h n)").bitcast(FP8X4),
-                                  scales=sc[:].rearrange("p h n -> p (h n)"),
-                                  in_=q_inter[b, w][:].rearrange("p h n t -> p (h n t)"))
-            q_codes[b, w], q_scales[b, w] = cd, sc
+        def q_quant(b, w, i):
+            nc.vector.quantize_mx(out=q_codes[b, w][:, i].rearrange("p h n -> p (h n)").bitcast(FP8X4),
+                                  scales=q_scales[b, w][:, i].rearrange("p h n -> p (h n)"),
+                                  in_=q_inter[b, w][:, i].rearrange("p h n t -> p (h n t)"))
 
         z_bank, z_ss, z_rstd, z_res = {}, {}, {}, {}
 
         def z_mult(b, w, i):
             bank = psum.tile([P, E], F32, name="zi_bank", bufs=4)
-            cols = slice(i * P, (i + 1) * P)
             for h in range(2):
                 nc.tensor.matmul_mx(
                     out=bank[:],
-                    lhsT=q_codes[b, w][:, h, cols].bitcast(FP8X4),
-                    lhsT_scale=q_scales[b, w][:, h, cols],
+                    lhsT=q_codes[b, w][:, i, h].bitcast(FP8X4),
+                    lhsT_scale=q_scales[b, w][:, i, h],
                     rhs=m_codes[b, h][:].bitcast(FP8X4),
                     rhs_scale=m_scales[b, h][:],
                     start=(h == 0), stop=(h == 1))
@@ -240,191 +249,199 @@ def tile_cosformernormlinearattention_kernel(tc, q, k, v_bytes, v_scale, gc, gt,
             else:
                 nc.scalar.activation(out=res[:], in_=z_bank[b, w, i][:], func=ACT.Copy, scale=z_rstd[b, w, i][:])
             nc.sync.dma_start(out=out[b].rearrange("(w i r) e -> w i r e", i=2, r=P)[w, i], in_=res[:])
-
-        scale_unit(0, 2, 0)
-        scale_unit(0, 1, 0)
+        scale_v(0, 0, 0, "V")
+        scale_v(0, 0, 1, "S")
+        gate_chunk(1)
+        scale_v(0, 1, 0, "S")
+        scale_k(0, 1, 0)
         turn_planes((0, 2, 0), 0)
-        scale_unit(0, 0, 0)
-        interleave((0, 1, 0), "S")
-        gate_chunk(2)
-        turn_planes((0, 0, 0), 0)
-        scale_unit(0, 1, 1)
-        q_turn(0, 0)
-        scale_unit(0, 2, 1)
-        interleave((0, 1, 1), "S")
-        q_turn(0, 2)
-        quant_unit((0, 1, 0))
-        scale_unit(1, 2, 0)
-        turn_planes((0, 0, 0), 1)
-        scale_unit(1, 1, 0)
-        copy_planes((0, 2, 0), 0, "S")
+        scale_k(0, 0, 0)
         turn_planes((0, 2, 0), 1)
-        scale_unit(1, 2, 1)
-        copy_planes((0, 0, 0), 0, "S")
+        scale_v(0, 1, 1, "S")
+        interleave((0, 1, 0), "V")
+        q_turn(0, 0)
+        copy_planes((0, 2, 0), 0, "S")
+        interleave((0, 0, 0), "V")
         interleave((0, 2, 1), "S")
+        q_turn(0, 2)
+        scale_k(0, 0, 1)
+        quant_unit((0, 1, 0))
+        scale_k(1, 1, 0)
+        scale_v(1, 0, 1, "S")
+        scale_k(1, 0, 0)
         turn_planes((1, 1, 0), 1)
-        scale_unit(1, 1, 1)
-        gate_chunk(3)
+        scale_v(1, 1, 1, "V")
+        interleave((0, 0, 1), "S")
+        scale_k(1, 0, 1)
+        turn_planes((1, 1, 0), 0)
+        scale_k(1, 1, 1)
+        scale_k(0, 1, 1)
         turn_planes((1, 1, 1), 0)
-        scale_unit(0, 0, 1)
+        quant_unit((0, 0, 0))
         copy_planes((0, 2, 0), 1, "S")
+        quant_unit((0, 0, 1))
+        scale_v(1, 1, 0, "S")
+        turn_planes((1, 1, 1), 1)
+        quant_unit((0, 2, 0))
         quant_unit((0, 2, 1))
         copy_planes((1, 1, 1), 0, "S")
-        turn_planes((1, 1, 0), 0)
-        quant_unit((0, 2, 0))
-        interleave((0, 0, 1), "S")
-        quant_unit((0, 1, 1))
-        turn_planes((1, 2, 1), 0)
-        q_gate(0, 0, 0)
-        m_mult(0, 1, 3)
         gate_chunk(0)
+        interleave((0, 1, 1), "S")
+        m_mult(0, 0, 0)
+        m_mult(0, 0, 3)
+        gate_chunk(2)
+        turn_planes((1, 2, 1), 0)
+        gate_chunk(3)
+        m_copy(0, 0, 0, "S")
+        m_copy(0, 0, 3, "S")
+        quant_unit((0, 1, 1))
+        m_mult(0, 0, 1)
+        scale_v(1, 0, 0, "S")
+        q_gate(0, 2, 0)
+        m_mult(0, 1, 3)
+        m_copy(0, 0, 1, "S")
+        q_gate(0, 0, 0)
+        m_copy(0, 1, 3, "S")
+        m_mult(0, 0, 2)
+        copy_planes((1, 1, 1), 1, "S")
+        interleave((1, 2, 0), "V")
+        m_mult(0, 1, 2)
+        copy_planes((1, 2, 1), 0, "S")
+        m_copy(0, 0, 2, "S")
+        turn_planes((1, 2, 1), 1)
+        quant_unit((1, 1, 1))
+        m_copy(0, 1, 2, "S")
+        m_quant(0, 0)
         copy_planes((1, 1, 0), 0, "S")
         m_mult(0, 1, 1)
-        quant_unit((0, 0, 1))
-        m_copy(0, 1, 3, "S")
+        quant_unit((1, 2, 0))
+        copy_planes((1, 2, 1), 1, "S")
+        m_mult(0, 1, 0)
         q_gate(0, 0, 1)
         copy_planes((1, 1, 0), 1, "S")
-        turn_planes((1, 2, 1), 1)
         m_copy(0, 1, 1, "S")
-        quant_unit((1, 1, 0))
-        copy_planes((1, 2, 1), 0, "S")
-        m_mult(0, 1, 0)
-        copy_planes((0, 0, 0), 1, "S")
-        q_quant(0, 0)
-        q_turn(1, 3)
-        copy_planes((1, 2, 1), 1, "S")
-        scale_unit(1, 0, 1)
-        m_copy(0, 1, 0, "S")
-        quant_unit((0, 0, 0))
-        m_mult(0, 1, 2)
-        interleave((1, 2, 0), "S")
         quant_unit((1, 2, 1))
-        interleave((1, 0, 1), "V")
-        m_mult(0, 0, 1)
-        turn_planes((1, 1, 1), 1)
-        m_copy(0, 1, 2, "V")
-        m_copy(0, 0, 1, "S")
-        quant_unit((1, 0, 1))
-        m_mult(0, 0, 3)
-        copy_planes((1, 1, 1), 1, "S")
-        quant_unit((1, 2, 0))
-        m_mult(0, 0, 0)
-        m_quant(0, 1)
-        m_copy(0, 0, 3, "S")
-        quant_unit((1, 1, 1))
-        m_mult(0, 0, 2)
-        m_copy(0, 0, 0, "S")
-        gate_chunk(1)
-        m_mult(1, 1, 1)
-        m_copy(0, 0, 2, "S")
-        scale_unit(1, 0, 0)
-        q_gate(0, 2, 0)
-        m_mult(1, 1, 3)
-        m_copy(1, 1, 1, "S")
-        interleave((1, 0, 0), "S")
-        m_mult(1, 1, 2)
-        m_quant(0, 0)
-        q_gate(0, 2, 1)
-        z_mult(0, 0, 1)
-        z_mult(0, 0, 0)
-        q_gate(1, 3, 0)
-        m_copy(1, 1, 3, "S")
+        m_copy(0, 1, 0, "S")
         q_turn(0, 3)
-        quant_unit((1, 0, 0))
-        m_copy(1, 1, 2, "S")
-        z_square(0, 0, 1)
-        q_gate(1, 3, 1)
-        m_mult(1, 0, 2)
-        z_square(0, 0, 0)
+        q_quant(0, 0, 0)
+        interleave((1, 0, 0), "S")
+        quant_unit((1, 1, 0))
+        m_quant(0, 1)
+        m_mult(1, 1, 2)
         q_gate(0, 3, 0)
-        m_mult(1, 0, 0)
-        z_rsqrt(0, 0, 1)
-        m_copy(1, 0, 2, "S")
-        z_rsqrt(0, 0, 0)
-        q_turn(0, 1)
-        z_scale(0, 0, 1, "S")
-        q_quant(0, 2)
-        z_scale(0, 0, 0, "S")
-        q_gate(0, 3, 1)
-        m_copy(1, 0, 0, "S")
-        z_mult(0, 2, 1)
-        q_gate(0, 1, 0)
-        m_mult(1, 0, 1)
-        z_square(0, 2, 1)
-        m_mult(1, 0, 3)
-        q_quant(0, 3)
-        m_copy(1, 0, 1, "S")
-        q_gate(0, 1, 1)
-        z_rsqrt(0, 2, 1)
-        q_turn(1, 2)
-        m_copy(1, 0, 3, "S")
-        q_quant(1, 3)
-        z_scale(0, 2, 1, "S")
+        m_mult(1, 1, 3)
+        q_gate(0, 2, 1)
+        m_copy(1, 1, 2, "S")
+        z_mult(0, 0, 0)
+        m_copy(1, 1, 3, "S")
         m_mult(1, 1, 0)
-        m_quant(1, 0)
-        q_gate(1, 2, 0)
+        q_gate(0, 3, 1)
+        z_square(0, 0, 0)
+        m_mult(1, 1, 1)
+        interleave((1, 0, 1), "S")
+        quant_unit((1, 0, 0))
+        q_turn(1, 3)
+        q_quant(0, 3, 1)
+        q_quant(0, 2, 0)
+        q_quant(0, 3, 0)
         z_mult(0, 3, 1)
-        z_mult(0, 2, 0)
-        q_quant(0, 1)
-        z_square(0, 3, 1)
-        q_gate(1, 2, 1)
+        q_quant(0, 0, 1)
+        q_gate(1, 3, 0)
         z_mult(0, 3, 0)
-        z_square(0, 2, 0)
-        z_mult(0, 1, 0)
-        z_rsqrt(0, 3, 1)
+        m_copy(1, 1, 1, "S")
+        z_square(0, 3, 1)
+        z_mult(0, 2, 0)
+        quant_unit((1, 0, 1))
         z_square(0, 3, 0)
-        m_copy(1, 1, 0, "V")
-        q_turn(1, 0)
-        q_quant(1, 2)
-        z_scale(0, 3, 1, "S")
-        m_quant(1, 1)
+        q_turn(0, 1)
+        q_gate(1, 3, 1)
+        z_rsqrt(0, 3, 1)
+        m_copy(1, 1, 0, "S")
+        m_mult(1, 0, 0)
+        q_quant(0, 2, 1)
         z_rsqrt(0, 3, 0)
-        z_square(0, 1, 0)
-        z_mult(0, 1, 1)
-        z_scale(0, 3, 0, "S")
-        q_gate(1, 0, 0)
-        z_rsqrt(0, 1, 0)
-        q_turn(1, 1)
+        z_rsqrt(0, 0, 0)
+        z_square(0, 2, 0)
+        q_gate(0, 1, 0)
+        m_mult(1, 0, 3)
+        z_scale(0, 0, 0, "S")
+        m_copy(1, 0, 0, "S")
+        m_quant(1, 1)
+        q_turn(1, 0)
+        m_copy(1, 0, 3, "S")
+        q_quant(1, 3, 1)
+        q_gate(0, 1, 1)
         z_rsqrt(0, 2, 0)
-        z_square(0, 1, 1)
-        z_scale(0, 2, 0, "V")
-        z_scale(0, 1, 0, "S")
+        z_scale(0, 3, 0, "S")
+        z_mult(0, 2, 1)
+        z_scale(0, 3, 1, "S")
+        m_mult(1, 0, 2)
+        q_gate(1, 0, 0)
+        z_square(0, 2, 1)
+        z_mult(0, 0, 1)
+        m_copy(1, 0, 2, "S")
+        q_quant(0, 1, 0)
+        m_mult(1, 0, 1)
+        q_quant(0, 1, 1)
+        z_rsqrt(0, 2, 1)
+        z_square(0, 0, 1)
         q_gate(1, 0, 1)
-        z_mult(1, 3, 1)
-        z_rsqrt(0, 1, 1)
-        z_scale(0, 1, 1, "S")
-        z_mult(1, 2, 1)
-        q_gate(1, 1, 0)
-        z_square(1, 3, 1)
-        z_mult(1, 2, 0)
-        z_square(1, 2, 1)
-        q_quant(1, 0)
-        z_mult(1, 3, 0)
-        z_rsqrt(1, 3, 1)
-        z_rsqrt(1, 2, 1)
-        z_scale(1, 3, 1, "V")
-        z_square(1, 2, 0)
-        q_gate(1, 1, 1)
-        z_scale(1, 2, 1, "S")
-        z_mult(1, 0, 1)
-        z_rsqrt(1, 2, 0)
-        z_square(1, 3, 0)
+        z_mult(0, 1, 0)
+        z_scale(0, 2, 1, "S")
+        q_turn(1, 2)
+        m_copy(1, 0, 1, "V")
+        z_rsqrt(0, 0, 1)
+        z_scale(0, 2, 0, "S")
+        q_quant(1, 0, 0)
+        z_square(0, 1, 0)
+        m_quant(1, 0)
+        z_mult(0, 1, 1)
+        z_scale(0, 0, 1, "S")
+        q_gate(1, 2, 0)
         z_mult(1, 0, 0)
-        z_scale(1, 2, 0, "S")
-        q_quant(1, 1)
-        z_rsqrt(1, 3, 0)
-        z_square(1, 0, 1)
-        z_mult(1, 1, 0)
-        z_scale(1, 3, 0, "V")
+        z_rsqrt(0, 1, 0)
+        z_square(0, 1, 1)
+        q_turn(1, 1)
+        q_quant(1, 0, 1)
+        z_scale(0, 1, 0, "S")
+        q_gate(1, 2, 1)
+        z_rsqrt(0, 1, 1)
         z_square(1, 0, 0)
-        z_mult(1, 1, 1)
-        z_rsqrt(1, 0, 1)
-        z_square(1, 1, 0)
-        z_scale(1, 0, 1, "V")
+        z_mult(1, 0, 1)
+        q_gate(1, 1, 0)
+        z_scale(0, 1, 1, "S")
+        z_mult(1, 3, 1)
         z_rsqrt(1, 0, 0)
+        z_square(1, 0, 1)
+        q_quant(1, 2, 1)
+        z_scale(1, 0, 0, "S")
+        q_gate(1, 1, 1)
+        z_mult(1, 2, 1)
+        z_rsqrt(1, 0, 1)
+        z_square(1, 3, 1)
+        q_quant(1, 2, 0)
+        z_scale(1, 0, 1, "S")
+        q_quant(1, 1, 0)
+        z_mult(1, 2, 0)
+        q_quant(1, 1, 1)
+        z_rsqrt(1, 3, 1)
+        z_square(1, 2, 1)
+        z_scale(1, 3, 1, "V")
+        z_mult(1, 1, 0)
+        q_quant(1, 3, 0)
+        z_rsqrt(1, 2, 1)
+        z_square(1, 2, 0)
+        z_mult(1, 1, 1)
+        z_scale(1, 2, 1, "V")
+        z_square(1, 1, 0)
+        z_mult(1, 3, 0)
+        z_rsqrt(1, 2, 0)
         z_square(1, 1, 1)
-        z_scale(1, 0, 0, "V")
+        z_scale(1, 2, 0, "V")
         z_rsqrt(1, 1, 0)
-        z_rsqrt(1, 1, 1)
+        z_square(1, 3, 0)
         z_scale(1, 1, 0, "V")
+        z_rsqrt(1, 1, 1)
+        z_rsqrt(1, 3, 0)
         z_scale(1, 1, 1, "S")
+        z_scale(1, 3, 0, "V")

@@ -35,8 +35,8 @@ def tile_cosformernormlinearattention_kernel(tc, q, k, v_bytes, v_scale, gc, gt,
         gt_col = const.tile([P, G, T], BF16, name="gt_col")
         gc_col = const.tile([P, T], BF16, name="gc_col")
         vs_col = const.tile([P, G, T], F32, name="vs_col")
-        nc.scalar.dma_start(out=gt_col[:], in_=gt.rearrange("(g p t) -> p g t", p=P, t=T))
         nc.scalar.dma_start(out=vs_col[:], in_=v_scale.rearrange("o (g p t) x -> p (o g) (t x)", p=P, t=T))
+        nc.sync.dma_start(out=gt_col[:], in_=gt.rearrange("(g p t) -> p g t", p=P, t=T))
         nc.scalar.dma_start(out=gc_col[:], in_=gc.rearrange("(p t) -> p t", t=T))
 
         k_raw, v_raw, q_raw = {}, {}, {}
@@ -76,9 +76,10 @@ def tile_cosformernormlinearattention_kernel(tc, q, k, v_bytes, v_scale, gc, gt,
         sin_row = const.tile([P, N + 1], F32, name="sin_row")
         nc.scalar.activation(out=sin_row[:], in_=idx_row[:], func=ACT.Sin, scale=step)
 
+        warm = const.tile([P, 1], F32, name="warm")
+        nc.scalar.activation(out=warm[:], in_=sin_row[:, N:N + 1], func=ACT.Abs_reciprocal_sqrt)
+
         kscale = const.tile([P, 2, G, T], F32, name="kscale")
-        for h in range(2):
-            nc.vector.tensor_tensor(out=kscale[:, h], in0=trig_col[:, h], in1=gt_col[:], op=ALU.mult)
         gate = const.tile([P, N + 1, T], F32, name="gate")
 
         def gate_chunk(i):
@@ -125,8 +126,8 @@ def tile_cosformernormlinearattention_kernel(tc, q, k, v_bytes, v_scale, gc, gt,
                 dst = it[:].rearrange("p (c i t) -> p c t i", i=4, t=T)
                 src = pl[:].rearrange("p t (c i) -> p c t i", i=4)
             else:
-                dst = it[:].rearrange("p (s m t) -> p m t s", s=4, t=T)
-                src = pl[:].rearrange("p t (m s) -> p m t s", s=4)
+                dst = it[:].rearrange("p (s c i t) -> p s c t i", s=4, i=4, t=T)
+                src = pl[:].rearrange("p t (c i s) -> p s c t i", s=4, i=4)
             if eng == "V":
                 nc.vector.tensor_copy(out=dst, in_=src)
             else:
@@ -149,6 +150,16 @@ def tile_cosformernormlinearattention_kernel(tc, q, k, v_bytes, v_scale, gc, gt,
             it = inter_tile(u)
             (nc.vector.tensor_copy if eng == "V" else nc.scalar.copy)(
                 out=it[:, a * 1024:(a + 1) * 1024], in_=i_bank[u, a][:].rearrange("p j d -> p (j d)"))
+
+        def interleave_on_gpsimd(u, a):
+            it = inter_tile(u)
+            for s in (2 * a, 2 * a + 1):
+                if u[1] == 2:
+                    src = planes[u][:].rearrange("p t (s m) -> p s m t", s=4)[:, s]
+                else:
+                    src = planes[u][:].rearrange("p t (m s) -> p s m t", s=4)[:, s]
+                nc.gpsimd.tensor_scalar(out=it[:, s * D:(s + 1) * D].rearrange("p (m t) -> p m t", t=T), in0=src,
+                                        scalar1=1.0, scalar2=0.0, op0=ALU.mult, op1=ALU.add)
 
         def quant_unit(u):
             cd = keep.tile([P, D], U32, name="codes%d%d%d" % u, align_bytes=64)
@@ -249,199 +260,201 @@ def tile_cosformernormlinearattention_kernel(tc, q, k, v_bytes, v_scale, gc, gt,
             else:
                 nc.scalar.activation(out=res[:], in_=z_bank[b, w, i][:], func=ACT.Copy, scale=z_rstd[b, w, i][:])
             nc.sync.dma_start(out=out[b].rearrange("(w i r) e -> w i r e", i=2, r=P)[w, i], in_=res[:])
+        scale_v(0, 0, 1, "V")
         scale_v(0, 0, 0, "V")
-        scale_v(0, 0, 1, "S")
-        gate_chunk(1)
-        scale_v(0, 1, 0, "S")
-        scale_k(0, 1, 0)
-        turn_planes((0, 2, 0), 0)
+        for h in range(2):
+            nc.vector.tensor_tensor(out=kscale[:, h], in0=trig_col[:, h], in1=gt_col[:], op=ALU.mult)
         scale_k(0, 0, 0)
-        turn_planes((0, 2, 0), 1)
-        scale_v(0, 1, 1, "S")
-        interleave((0, 1, 0), "V")
-        q_turn(0, 0)
-        copy_planes((0, 2, 0), 0, "S")
-        interleave((0, 0, 0), "V")
-        interleave((0, 2, 1), "S")
-        q_turn(0, 2)
-        scale_k(0, 0, 1)
-        quant_unit((0, 1, 0))
-        scale_k(1, 1, 0)
-        scale_v(1, 0, 1, "S")
-        scale_k(1, 0, 0)
-        turn_planes((1, 1, 0), 1)
-        scale_v(1, 1, 1, "V")
-        interleave((0, 0, 1), "S")
-        scale_k(1, 0, 1)
-        turn_planes((1, 1, 0), 0)
-        scale_k(1, 1, 1)
-        scale_k(0, 1, 1)
-        turn_planes((1, 1, 1), 0)
-        quant_unit((0, 0, 0))
-        copy_planes((0, 2, 0), 1, "S")
-        quant_unit((0, 0, 1))
-        scale_v(1, 1, 0, "S")
-        turn_planes((1, 1, 1), 1)
-        quant_unit((0, 2, 0))
-        quant_unit((0, 2, 1))
-        copy_planes((1, 1, 1), 0, "S")
-        gate_chunk(0)
-        interleave((0, 1, 1), "S")
-        m_mult(0, 0, 0)
-        m_mult(0, 0, 3)
-        gate_chunk(2)
-        turn_planes((1, 2, 1), 0)
+        interleave((0, 2, 0), "S")
         gate_chunk(3)
-        m_copy(0, 0, 0, "S")
-        m_copy(0, 0, 3, "S")
-        quant_unit((0, 1, 1))
-        m_mult(0, 0, 1)
-        scale_v(1, 0, 0, "S")
-        q_gate(0, 2, 0)
-        m_mult(0, 1, 3)
-        m_copy(0, 0, 1, "S")
+        scale_k(0, 1, 0)
+        q_turn(0, 0)
+        gate_chunk(0)
+        scale_v(0, 1, 0, "S")
+        q_turn(0, 2)
+        quant_unit((0, 2, 0))
+        scale_v(0, 1, 1, "S")
+        scale_k(0, 0, 1)
+        scale_v(1, 0, 0, "V")
+        turn_planes((0, 0, 1), 0)
+        interleave((0, 0, 0), "S")
+        scale_k(0, 1, 1)
         q_gate(0, 0, 0)
-        m_copy(0, 1, 3, "S")
-        m_mult(0, 0, 2)
-        copy_planes((1, 1, 1), 1, "S")
-        interleave((1, 2, 0), "V")
-        m_mult(0, 1, 2)
-        copy_planes((1, 2, 1), 0, "S")
-        m_copy(0, 0, 2, "S")
-        turn_planes((1, 2, 1), 1)
-        quant_unit((1, 1, 1))
-        m_copy(0, 1, 2, "S")
-        m_quant(0, 0)
-        copy_planes((1, 1, 0), 0, "S")
-        m_mult(0, 1, 1)
-        quant_unit((1, 2, 0))
-        copy_planes((1, 2, 1), 1, "S")
-        m_mult(0, 1, 0)
+        interleave_on_gpsimd((0, 2, 1), 0)
+        turn_planes((0, 0, 1), 1)
+        copy_planes((0, 0, 1), 0, "V")
+        turn_planes((0, 1, 1), 0)
+        scale_k(1, 0, 1)
+        scale_v(1, 1, 1, "S")
+        turn_planes((0, 1, 1), 1)
+        copy_planes((0, 0, 1), 1, "V")
+        interleave_on_gpsimd((0, 2, 1), 1)
         q_gate(0, 0, 1)
-        copy_planes((1, 1, 0), 1, "S")
-        m_copy(0, 1, 1, "S")
-        quant_unit((1, 2, 1))
-        m_copy(0, 1, 0, "S")
+        interleave((0, 1, 0), "S")
+        quant_unit((0, 0, 0))
         q_turn(0, 3)
-        q_quant(0, 0, 0)
-        interleave((1, 0, 0), "S")
-        quant_unit((1, 1, 0))
-        m_quant(0, 1)
-        m_mult(1, 1, 2)
-        q_gate(0, 3, 0)
-        m_mult(1, 1, 3)
-        q_gate(0, 2, 1)
-        m_copy(1, 1, 2, "S")
-        z_mult(0, 0, 0)
-        m_copy(1, 1, 3, "S")
-        m_mult(1, 1, 0)
-        q_gate(0, 3, 1)
-        z_square(0, 0, 0)
-        m_mult(1, 1, 1)
-        interleave((1, 0, 1), "S")
-        quant_unit((1, 0, 0))
-        q_turn(1, 3)
-        q_quant(0, 3, 1)
-        q_quant(0, 2, 0)
-        q_quant(0, 3, 0)
-        z_mult(0, 3, 1)
+        quant_unit((0, 2, 1))
+        quant_unit((0, 0, 1))
+        copy_planes((0, 1, 1), 0, "S")
+        quant_unit((0, 1, 0))
+        scale_v(1, 0, 1, "S")
+        m_mult(0, 0, 1)
         q_quant(0, 0, 1)
-        q_gate(1, 3, 0)
-        z_mult(0, 3, 0)
-        m_copy(1, 1, 1, "S")
-        z_square(0, 3, 1)
-        z_mult(0, 2, 0)
-        quant_unit((1, 0, 1))
-        z_square(0, 3, 0)
+        gate_chunk(1)
+        m_mult(0, 0, 2)
+        copy_planes((0, 1, 1), 1, "S")
+        interleave((1, 2, 0), "V")
+        m_copy(0, 0, 1, "S")
+        m_copy(0, 0, 2, "S")
+        m_mult(0, 0, 3)
+        scale_v(1, 1, 0, "S")
+        quant_unit((0, 1, 1))
+        m_mult(0, 0, 0)
+        quant_unit((1, 2, 0))
+        m_copy(0, 0, 3, "S")
+        scale_k(1, 0, 0)
+        turn_planes((1, 2, 1), 0)
+        m_copy(0, 0, 0, "S")
+        scale_k(1, 1, 1)
+        interleave((1, 0, 1), "S")
+        m_mult(0, 1, 0)
+        q_gate(0, 3, 0)
+        interleave_on_gpsimd((1, 0, 0), 0)
+        m_mult(0, 1, 3)
+        copy_planes((1, 2, 1), 0, "V")
+        turn_planes((1, 2, 1), 1)
+        m_quant(0, 0)
+        m_copy(0, 1, 0, "S")
+        q_gate(0, 3, 1)
+        interleave_on_gpsimd((1, 0, 0), 1)
+        m_copy(0, 1, 3, "S")
+        m_mult(0, 1, 2)
+        copy_planes((1, 2, 1), 1, "V")
+        interleave((1, 1, 1), "S")
+        m_mult(0, 1, 1)
+        q_quant(0, 3, 1)
+        quant_unit((1, 2, 1))
         q_turn(0, 1)
-        q_gate(1, 3, 1)
-        z_rsqrt(0, 3, 1)
-        m_copy(1, 1, 0, "S")
+        quant_unit((1, 0, 0))
+        quant_unit((1, 0, 1))
+        m_copy(0, 1, 2, "S")
+        q_quant(0, 0, 0)
+        quant_unit((1, 1, 1))
+        m_copy(0, 1, 1, "S")
+        m_mult(1, 0, 1)
+        q_quant(0, 3, 0)
+        m_quant(0, 1)
+        m_mult(1, 0, 3)
+        m_copy(1, 0, 1, "S")
+        gate_chunk(2)
+        z_mult(0, 3, 1)
+        m_copy(1, 0, 3, "S")
+        scale_k(1, 1, 0)
+        m_mult(1, 0, 2)
+        z_square(0, 3, 1)
+        q_gate(0, 1, 0)
+        z_mult(0, 0, 0)
+        interleave_on_gpsimd((1, 1, 0), 0)
+        m_copy(1, 0, 2, "S")
         m_mult(1, 0, 0)
+        q_gate(0, 2, 0)
+        z_rsqrt(0, 3, 1)
+        z_square(0, 0, 0)
+        z_mult(0, 0, 1)
+        z_scale(0, 3, 1, "S")
+        q_gate(0, 1, 1)
+        interleave_on_gpsimd((1, 1, 0), 1)
+        z_mult(0, 3, 0)
+        z_rsqrt(0, 0, 0)
+        m_copy(1, 0, 0, "S")
+        z_scale(0, 0, 0, "S")
+        q_gate(0, 2, 1)
+        q_turn(1, 1)
+        z_square(0, 0, 1)
+        q_quant(0, 1, 1)
+        z_square(0, 3, 0)
+        q_quant(0, 1, 0)
+        q_turn(1, 0)
+        q_quant(0, 2, 0)
+        z_rsqrt(0, 0, 1)
         q_quant(0, 2, 1)
         z_rsqrt(0, 3, 0)
-        z_rsqrt(0, 0, 0)
-        z_square(0, 2, 0)
-        q_gate(0, 1, 0)
-        m_mult(1, 0, 3)
-        z_scale(0, 0, 0, "S")
-        m_copy(1, 0, 0, "S")
-        m_quant(1, 1)
-        q_turn(1, 0)
-        m_copy(1, 0, 3, "S")
-        q_quant(1, 3, 1)
-        q_gate(0, 1, 1)
-        z_rsqrt(0, 2, 0)
-        z_scale(0, 3, 0, "S")
-        z_mult(0, 2, 1)
-        z_scale(0, 3, 1, "S")
-        m_mult(1, 0, 2)
-        q_gate(1, 0, 0)
-        z_square(0, 2, 1)
-        z_mult(0, 0, 1)
-        m_copy(1, 0, 2, "S")
-        q_quant(0, 1, 0)
-        m_mult(1, 0, 1)
-        q_quant(0, 1, 1)
-        z_rsqrt(0, 2, 1)
-        z_square(0, 0, 1)
-        q_gate(1, 0, 1)
-        z_mult(0, 1, 0)
-        z_scale(0, 2, 1, "S")
-        q_turn(1, 2)
-        m_copy(1, 0, 1, "V")
-        z_rsqrt(0, 0, 1)
-        z_scale(0, 2, 0, "S")
-        q_quant(1, 0, 0)
-        z_square(0, 1, 0)
-        m_quant(1, 0)
-        z_mult(0, 1, 1)
         z_scale(0, 0, 1, "S")
-        q_gate(1, 2, 0)
-        z_mult(1, 0, 0)
-        z_rsqrt(0, 1, 0)
-        z_square(0, 1, 1)
-        q_turn(1, 1)
-        q_quant(1, 0, 1)
-        z_scale(0, 1, 0, "S")
-        q_gate(1, 2, 1)
-        z_rsqrt(0, 1, 1)
-        z_square(1, 0, 0)
-        z_mult(1, 0, 1)
+        quant_unit((1, 1, 0))
+        z_mult(0, 2, 0)
+        z_scale(0, 3, 0, "S")
+        m_quant(1, 0)
+        m_mult(1, 1, 1)
         q_gate(1, 1, 0)
-        z_scale(0, 1, 1, "S")
-        z_mult(1, 3, 1)
-        z_rsqrt(1, 0, 0)
-        z_square(1, 0, 1)
-        q_quant(1, 2, 1)
-        z_scale(1, 0, 0, "S")
+        z_square(0, 2, 0)
+        m_mult(1, 1, 0)
+        m_copy(1, 1, 1, "S")
+        q_gate(1, 0, 0)
+        z_mult(0, 1, 1)
+        z_rsqrt(0, 2, 0)
+        m_copy(1, 1, 0, "S")
+        m_mult(1, 1, 3)
         q_gate(1, 1, 1)
-        z_mult(1, 2, 1)
-        z_rsqrt(1, 0, 1)
-        z_square(1, 3, 1)
-        q_quant(1, 2, 0)
-        z_scale(1, 0, 1, "S")
-        q_quant(1, 1, 0)
-        z_mult(1, 2, 0)
+        z_scale(0, 2, 0, "S")
+        z_square(0, 1, 1)
+        m_mult(1, 1, 2)
+        q_gate(1, 0, 1)
+        m_copy(1, 1, 3, "S")
+        z_mult(0, 1, 0)
+        m_copy(1, 1, 2, "S")
         q_quant(1, 1, 1)
-        z_rsqrt(1, 3, 1)
-        z_square(1, 2, 1)
-        z_scale(1, 3, 1, "V")
+        q_turn(1, 3)
+        q_quant(1, 0, 1)
+        z_square(0, 1, 0)
+        m_quant(1, 1)
+        z_rsqrt(0, 1, 1)
+        z_mult(0, 2, 1)
+        q_quant(1, 0, 0)
+        z_scale(0, 1, 1, "S")
+        q_gate(1, 3, 0)
+        z_mult(1, 0, 1)
+        z_rsqrt(0, 1, 0)
+        z_square(0, 2, 1)
+        z_mult(1, 1, 1)
+        z_scale(0, 1, 0, "V")
+        z_square(1, 0, 1)
+        q_gate(1, 3, 1)
+        q_turn(1, 2)
+        z_rsqrt(0, 2, 1)
+        z_square(1, 1, 1)
+        q_quant(1, 1, 0)
+        z_rsqrt(1, 0, 1)
+        z_scale(0, 2, 1, "S")
+        z_mult(1, 0, 0)
+        q_quant(1, 3, 1)
+        q_gate(1, 2, 0)
+        z_scale(1, 0, 1, "S")
+        z_mult(1, 3, 1)
+        z_rsqrt(1, 1, 1)
+        z_square(1, 0, 0)
         z_mult(1, 1, 0)
         q_quant(1, 3, 0)
-        z_rsqrt(1, 2, 1)
-        z_square(1, 2, 0)
-        z_mult(1, 1, 1)
-        z_scale(1, 2, 1, "V")
-        z_square(1, 1, 0)
-        z_mult(1, 3, 0)
-        z_rsqrt(1, 2, 0)
-        z_square(1, 1, 1)
-        z_scale(1, 2, 0, "V")
-        z_rsqrt(1, 1, 0)
-        z_square(1, 3, 0)
-        z_scale(1, 1, 0, "V")
-        z_rsqrt(1, 1, 1)
-        z_rsqrt(1, 3, 0)
         z_scale(1, 1, 1, "S")
+        q_gate(1, 2, 1)
+        z_rsqrt(1, 0, 0)
+        z_square(1, 3, 1)
+        z_mult(1, 3, 0)
+        z_scale(1, 0, 0, "S")
+        q_quant(1, 2, 0)
+        q_quant(1, 2, 1)
+        z_rsqrt(1, 3, 1)
+        z_square(1, 3, 0)
+        z_mult(1, 2, 0)
+        z_scale(1, 3, 1, "V")
+        z_square(1, 1, 0)
+        z_mult(1, 2, 1)
+        z_rsqrt(1, 3, 0)
+        z_square(1, 2, 0)
         z_scale(1, 3, 0, "V")
+        z_rsqrt(1, 1, 0)
+        z_square(1, 2, 1)
+        z_scale(1, 1, 0, "V")
+        z_rsqrt(1, 2, 0)
+        z_rsqrt(1, 2, 1)
+        z_scale(1, 2, 0, "S")
+        z_scale(1, 2, 1, "V")

import math
from contextlib import ExitStack

import concourse.mybir as mybir
from concourse.masks import make_identity

B, N, D, E = 2, 1024, 512, 512
FLOPS = 2 * 4 * 2 * N * D * E
EPS = 1e-6

P = 128
T = 4
G = N // (P * T)
F32 = mybir.dt.float32
BF16 = mybir.dt.bfloat16
U32 = mybir.dt.uint32
U8 = mybir.dt.uint8
FP8 = mybir.dt.float8_e4m3fn
FP8X4 = mybir.dt.float8_e4m3fn_x4
ACT = mybir.ActivationFunctionType
ALU = mybir.AluOpType


def tile_cosformernormlinearattention_kernel(tc, q, k, v_bytes, v_scale, gc, gt, out):
    nc = tc.nc
    with ExitStack() as ctx:
        const = ctx.enter_context(tc.tile_pool(name="const", bufs=1))
        loads = ctx.enter_context(tc.tile_pool(name="loads", bufs=1))
        work = ctx.enter_context(tc.tile_pool(name="work", bufs=4))
        keep = ctx.enter_context(tc.tile_pool(name="keep", bufs=1))
        outp = ctx.enter_context(tc.tile_pool(name="outp", bufs=3))
        psum = ctx.enter_context(tc.psum_pool(name="psum", bufs=2))
        ctx.enter_context(tc.manual_schedule())

        gt_col = const.tile([P, G, T], BF16, name="gt_col")
        gc_col = const.tile([P, T], BF16, name="gc_col")
        vs_col = const.tile([P, G, T], F32, name="vs_col")
        nc.scalar.dma_start(out=vs_col[:], in_=v_scale.rearrange("o (g p t) x -> p (o g) (t x)", p=P, t=T))
        nc.sync.dma_start(out=gt_col[:], in_=gt.rearrange("(g p t) -> p g t", p=P, t=T))
        nc.scalar.dma_start(out=gc_col[:], in_=gc.rearrange("(p t) -> p t", t=T))

        k_raw, v_raw, q_raw = {}, {}, {}

        def load_kv(b, g):
            vt = loads.tile([P, T, E], U8, name="v_raw%d%d" % (b, g))
            nc.sync.dma_start(out=vt[:], in_=v_bytes[b].rearrange("(g p t) d -> g p t d", p=P, t=T)[g])
            kt = loads.tile([P, T, D], BF16, name="k_raw%d%d" % (b, g))
            nc.sync.dma_start(out=kt[:], in_=k[b].rearrange("(g p t) d -> g p t d", p=P, t=T)[g])
            k_raw[b, g], v_raw[b, g] = kt, vt

        def load_q(b, w):
            qt = loads.tile([P, 2, D], BF16, name="q_raw%d%d" % (b, w))
            nc.sync.dma_start(out=qt[:], in_=q[b].rearrange("(w i r) d -> w r i d", i=2, r=P)[w])
            q_raw[b, w] = qt

        for b in range(B):
            for g in range(G):
                load_kv(b, g)
            for w in range(4):
                load_q(b, w)

        idx_col = const.tile([P, 2, G, T], F32, name="idx_col")
        nc.gpsimd.iota(idx_col[:, 0], pattern=[[-512, G], [-1, T]], base=N, channel_multiplier=-T,
                       allow_small_or_imprecise_dtypes=True)
        nc.gpsimd.iota(idx_col[:, 1], pattern=[[512, G], [1, T]], base=0, channel_multiplier=T,
                       allow_small_or_imprecise_dtypes=True)
        idx_row = const.tile([P, N + 1], F32, name="idx_row")
        nc.gpsimd.iota(idx_row[:], pattern=[[1, N + 1]], base=0, channel_multiplier=0,
                       allow_small_or_imprecise_dtypes=True)
        ident = const.tile([P, P], BF16, name="ident")
        make_identity(nc, ident[:])

        step = math.pi / (2 * N)
        trig_col = const.tile([P, 2, G, T], F32, name="trig_col")
        nc.scalar.activation(out=trig_col[:], in_=idx_col[:], func=ACT.Sin, scale=step)
        sin_row = const.tile([P, N + 1], F32, name="sin_row")
        nc.scalar.activation(out=sin_row[:], in_=idx_row[:], func=ACT.Sin, scale=step)

        warm = const.tile([P, 1], F32, name="warm")
        nc.scalar.activation(out=warm[:], in_=sin_row[:, N:N + 1], func=ACT.Abs_reciprocal_sqrt)

        kscale = const.tile([P, 2, G, T], F32, name="kscale")
        gate = const.tile([P, N + 1, T], F32, name="gate")

        def gate_chunk(i):
            lo = i * 256
            hi = lo + 256 + (1 if i == 3 else 0)
            nc.vector.tensor_tensor(
                out=gate[:, lo:hi, :],
                in0=sin_row[:, lo:hi].unsqueeze(2).to_broadcast([P, hi - lo, T]),
                in1=gc_col[:].unsqueeze(1).to_broadcast([P, hi - lo, T]),
                op=ALU.mult)

        planes, inter, codes, scales = {}, {}, {}, {}

        def planes_tile(u):
            if u not in planes:
                planes[u] = work.tile([P, T, D], BF16, name="planes", bufs=8)
            return planes[u]

        def scale_k(b, kind, g):
            pl = planes_tile((b, kind, g))
            for t in range(T):
                nc.vector.tensor_scalar(out=pl[:, t], in0=k_raw[b, g][:, t], scalar1=0.0,
                                        scalar2=kscale[:, kind, g, t:t + 1], op0=ALU.max, op1=ALU.mult)

        def scale_v(b, g, half, eng):
            pl = planes_tile((b, 2, g))
            for t in (2 * half, 2 * half + 1):
                src = v_raw[b, g][:, t].bitcast(FP8)
                factor = vs_col[:, g, t:t + 1]
                if eng == "V":
                    nc.vector.tensor_scalar(out=pl[:, t], in0=src, scalar1=factor, scalar2=None, op0=ALU.mult)
                else:
                    nc.scalar.activation(out=pl[:, t], in_=src, func=ACT.Copy, scale=factor)

        def inter_tile(u):
            if u not in inter:
                inter[u] = work.tile([P, D * T], BF16, name="inter", align_bytes=64, bufs=6)
            return inter[u]

        def interleave(u, eng):
            it = inter_tile(u)
            pl = planes[u]
            if u[1] == 2:
                dst = it[:].rearrange("p (c i t) -> p c t i", i=4, t=T)
                src = pl[:].rearrange("p t (c i) -> p c t i", i=4)
            else:
                dst = it[:].rearrange("p (s c i t) -> p s c t i", s=4, i=4, t=T)
                src = pl[:].rearrange("p t (c i s) -> p s c t i", s=4, i=4)
            if eng == "V":
                nc.vector.tensor_copy(out=dst, in_=src)
            else:
                nc.scalar.copy(out=dst, in_=src)

        i_bank = {}

        def turn_planes(u, a):
            bank = psum.tile([P, 2, D], BF16, name="zi_bank", bufs=4)
            for j in range(2):
                s = 2 * a + j
                if u[1] == 2:
                    src = planes[u][:].rearrange("p t (s m) -> p s m t", s=4)[:, s]
                else:
                    src = planes[u][:].rearrange("p t (m s) -> p s m t", s=4)[:, s]
                nc.tensor.matmul(bank[:, j], lhsT=ident[:], rhs=src, start=True, stop=True)
            i_bank[u, a] = bank

        def copy_planes(u, a, eng):
            it = inter_tile(u)
            (nc.vector.tensor_copy if eng == "V" else nc.scalar.copy)(
                out=it[:, a * 1024:(a + 1) * 1024], in_=i_bank[u, a][:].rearrange("p j d -> p (j d)"))

        def interleave_on_gpsimd(u, a):
            it = inter_tile(u)
            for s in (2 * a, 2 * a + 1):
                if u[1] == 2:
                    src = planes[u][:].rearrange("p t (s m) -> p s m t", s=4)[:, s]
                else:
                    src = planes[u][:].rearrange("p t (m s) -> p s m t", s=4)[:, s]
                nc.gpsimd.tensor_scalar(out=it[:, s * D:(s + 1) * D].rearrange("p (m t) -> p m t", t=T), in0=src,
                                        scalar1=1.0, scalar2=0.0, op0=ALU.mult, op1=ALU.add)

        def quant_unit(u):
            cd = keep.tile([P, D], U32, name="codes%d%d%d" % u, align_bytes=64)
            sc = keep.tile([P, D], U8, name="scales%d%d%d" % u, align_bytes=64)
            nc.vector.quantize_mx(out=cd[:].bitcast(FP8X4), scales=sc[:], in_=inter[u][:])
            codes[u], scales[u] = cd, sc

        m_inter, m_codes, m_scales, m_bank = {}, {}, {}, {}

        def m_mult(b, h, eb):
            bank = psum.tile([P, T, P], F32, name="m_bank", bufs=2)
            es = slice(eb * P, (eb + 1) * P)
            for s in range(T):
                for g in range(G):
                    nc.tensor.matmul_mx(
                        out=bank[:, s],
                        lhsT=codes[b, h, g][:, s * P:(s + 1) * P].bitcast(FP8X4),
                        lhsT_scale=scales[b, h, g][:, s * P:(s + 1) * P],
                        rhs=codes[b, 2, g][:, es].bitcast(FP8X4),
                        rhs_scale=scales[b, 2, g][:, es],
                        start=(g == 0), stop=(g == G - 1))
            m_bank[b, h, eb] = bank

        def m_copy(b, h, eb, eng):
            if (b, h) not in m_inter:
                m_inter[b, h] = keep.tile([P, E, T], BF16, name="m_inter%d%d" % (b, h), align_bytes=64)
            dst = m_inter[b, h][:, eb * P:(eb + 1) * P, :]
            src = m_bank[b, h, eb][:].rearrange("p s e -> p e s")
            (nc.vector.tensor_copy if eng == "V" else nc.scalar.copy)(out=dst, in_=src)

        def m_quant(b, h):
            cd = keep.tile([P, E], U32, name="mcodes%d%d" % (b, h), align_bytes=64)
            sc = keep.tile([P, E], U8, name="mscales%d%d" % (b, h), align_bytes=64)
            nc.vector.quantize_mx(out=cd[:].bitcast(FP8X4), scales=sc[:],
                                  in_=m_inter[b, h][:].rearrange("p e s -> p (e s)"))
            m_codes[b, h], m_scales[b, h] = cd, sc

        q_turned, q_inter, q_codes, q_scales = {}, {}, {}, {}

        def q_turn(b, w):
            bank = psum.tile([P, T, 2, P], BF16, name="t_bank", bufs=2)
            for i in range(2):
                for t in range(T):
                    nc.tensor.transpose(bank[:, t, i], q_raw[b, w][:, i, t::T], ident[:])
            q_turned[b, w] = bank

        def q_gate(b, w, h):
            if (b, w) not in q_inter:
                q_inter[b, w] = work.tile([P, 2, 2, P, T], BF16, name="q_inter", align_bytes=64)
                q_codes[b, w] = work.tile([P, 2, 2, P], U32, name="q_codes", align_bytes=64)
                q_scales[b, w] = work.tile([P, 2, 2, P], U8, name="q_scales", align_bytes=64)
            src = q_turned[b, w][:].rearrange("p t i r -> p i r t")
            n0 = w * 256
            if h == 0:
                tab = gate[:, N - n0:N - n0 - 256:-1, :]
            else:
                tab = gate[:, n0:n0 + 256, :]
            nc.vector.scalar_tensor_tensor(out=q_inter[b, w][:, :, h], in0=src, scalar=0.0,
                                           in1=tab.rearrange("p (i r) t -> p i r t", i=2),
                                           op0=ALU.max, op1=ALU.mult)

        def q_quant(b, w, i):
            nc.vector.quantize_mx(out=q_codes[b, w][:, i].rearrange("p h n -> p (h n)").bitcast(FP8X4),
                                  scales=q_scales[b, w][:, i].rearrange("p h n -> p (h n)"),
                                  in_=q_inter[b, w][:, i].rearrange("p h n t -> p (h n t)"))

        z_bank, z_ss, z_rstd, z_res = {}, {}, {}, {}

        def z_mult(b, w, i):
            bank = psum.tile([P, E], F32, name="zi_bank", bufs=4)
            for h in range(2):
                nc.tensor.matmul_mx(
                    out=bank[:],
                    lhsT=q_codes[b, w][:, i, h].bitcast(FP8X4),
                    lhsT_scale=q_scales[b, w][:, i, h],
                    rhs=m_codes[b, h][:].bitcast(FP8X4),
                    rhs_scale=m_scales[b, h][:],
                    start=(h == 0), stop=(h == 1))
            z_bank[b, w, i] = bank

        def z_square(b, w, i):
            junk = outp.tile([P, E], BF16, name="junk")
            ss = outp.tile([P, 1], F32, name="ss")
            nc.scalar.activation(out=junk[:], in_=z_bank[b, w, i][:], func=ACT.Square, accum_out=ss[:])
            z_ss[b, w, i] = ss

        def z_rsqrt(b, w, i):
            rstd = outp.tile([P, 1], F32, name="rstd")
            nc.scalar.activation(out=rstd[:], in_=z_ss[b, w, i][:], func=ACT.Abs_reciprocal_sqrt,
                                 scale=1.0 / E, bias=EPS)
            z_rstd[b, w, i] = rstd

        def z_scale(b, w, i, eng):
            res = outp.tile([P, E], F32, name="res", bufs=6)
            if eng == "V":
                nc.vector.tensor_scalar(out=res[:], in0=z_bank[b, w, i][:], scalar1=z_rstd[b, w, i][:],
                                        scalar2=None, op0=ALU.mult)
            else:
                nc.scalar.activation(out=res[:], in_=z_bank[b, w, i][:], func=ACT.Copy, scale=z_rstd[b, w, i][:])
            nc.sync.dma_start(out=out[b].rearrange("(w i r) e -> w i r e", i=2, r=P)[w, i], in_=res[:])
        scale_v(0, 0, 1, "V")
        scale_v(0, 0, 0, "V")
        for h in range(2):
            nc.vector.tensor_tensor(out=kscale[:, h], in0=trig_col[:, h], in1=gt_col[:], op=ALU.mult)
        scale_k(0, 0, 0)
        interleave((0, 2, 0), "S")
        gate_chunk(3)
        scale_k(0, 1, 0)
        q_turn(0, 0)
        gate_chunk(0)
        scale_v(0, 1, 0, "S")
        q_turn(0, 2)
        quant_unit((0, 2, 0))
        scale_v(0, 1, 1, "S")
        scale_k(0, 0, 1)
        scale_v(1, 0, 0, "V")
        turn_planes((0, 0, 1), 0)
        interleave((0, 0, 0), "S")
        scale_k(0, 1, 1)
        q_gate(0, 0, 0)
        interleave_on_gpsimd((0, 2, 1), 0)
        turn_planes((0, 0, 1), 1)
        copy_planes((0, 0, 1), 0, "V")
        turn_planes((0, 1, 1), 0)
        scale_k(1, 0, 1)
        scale_v(1, 1, 1, "S")
        turn_planes((0, 1, 1), 1)
        copy_planes((0, 0, 1), 1, "V")
        interleave_on_gpsimd((0, 2, 1), 1)
        q_gate(0, 0, 1)
        interleave((0, 1, 0), "S")
        quant_unit((0, 0, 0))
        q_turn(0, 3)
        quant_unit((0, 2, 1))
        quant_unit((0, 0, 1))
        copy_planes((0, 1, 1), 0, "S")
        quant_unit((0, 1, 0))
        scale_v(1, 0, 1, "S")
        m_mult(0, 0, 1)
        q_quant(0, 0, 1)
        gate_chunk(1)
        m_mult(0, 0, 2)
        copy_planes((0, 1, 1), 1, "S")
        interleave((1, 2, 0), "V")
        m_copy(0, 0, 1, "S")
        m_copy(0, 0, 2, "S")
        m_mult(0, 0, 3)
        scale_v(1, 1, 0, "S")
        quant_unit((0, 1, 1))
        m_mult(0, 0, 0)
        quant_unit((1, 2, 0))
        m_copy(0, 0, 3, "S")
        scale_k(1, 0, 0)
        turn_planes((1, 2, 1), 0)
        m_copy(0, 0, 0, "S")
        scale_k(1, 1, 1)
        interleave((1, 0, 1), "S")
        m_mult(0, 1, 0)
        q_gate(0, 3, 0)
        interleave_on_gpsimd((1, 0, 0), 0)
        m_mult(0, 1, 3)
        copy_planes((1, 2, 1), 0, "V")
        turn_planes((1, 2, 1), 1)
        m_quant(0, 0)
        m_copy(0, 1, 0, "S")
        q_gate(0, 3, 1)
        interleave_on_gpsimd((1, 0, 0), 1)
        m_copy(0, 1, 3, "S")
        m_mult(0, 1, 2)
        copy_planes((1, 2, 1), 1, "V")
        interleave((1, 1, 1), "S")
        m_mult(0, 1, 1)
        q_quant(0, 3, 1)
        quant_unit((1, 2, 1))
        q_turn(0, 1)
        quant_unit((1, 0, 0))
        quant_unit((1, 0, 1))
        m_copy(0, 1, 2, "S")
        q_quant(0, 0, 0)
        quant_unit((1, 1, 1))
        m_copy(0, 1, 1, "S")
        m_mult(1, 0, 1)
        q_quant(0, 3, 0)
        m_quant(0, 1)
        m_mult(1, 0, 3)
        m_copy(1, 0, 1, "S")
        gate_chunk(2)
        z_mult(0, 3, 1)
        m_copy(1, 0, 3, "S")
        scale_k(1, 1, 0)
        m_mult(1, 0, 2)
        z_square(0, 3, 1)
        q_gate(0, 1, 0)
        z_mult(0, 0, 0)
        interleave_on_gpsimd((1, 1, 0), 0)
        m_copy(1, 0, 2, "S")
        m_mult(1, 0, 0)
        q_gate(0, 2, 0)
        z_rsqrt(0, 3, 1)
        z_square(0, 0, 0)
        z_mult(0, 0, 1)
        z_scale(0, 3, 1, "S")
        q_gate(0, 1, 1)
        interleave_on_gpsimd((1, 1, 0), 1)
        z_mult(0, 3, 0)
        z_rsqrt(0, 0, 0)
        m_copy(1, 0, 0, "S")
        z_scale(0, 0, 0, "S")
        q_gate(0, 2, 1)
        q_turn(1, 1)
        z_square(0, 0, 1)
        q_quant(0, 1, 1)
        z_square(0, 3, 0)
        q_quant(0, 1, 0)
        q_turn(1, 0)
        q_quant(0, 2, 0)
        z_rsqrt(0, 0, 1)
        q_quant(0, 2, 1)
        z_rsqrt(0, 3, 0)
        z_scale(0, 0, 1, "S")
        quant_unit((1, 1, 0))
        z_mult(0, 2, 0)
        z_scale(0, 3, 0, "S")
        m_quant(1, 0)
        m_mult(1, 1, 1)
        q_gate(1, 1, 0)
        z_square(0, 2, 0)
        m_mult(1, 1, 0)
        m_copy(1, 1, 1, "S")
        q_gate(1, 0, 0)
        z_mult(0, 1, 1)
        z_rsqrt(0, 2, 0)
        m_copy(1, 1, 0, "S")
        m_mult(1, 1, 3)
        q_gate(1, 1, 1)
        z_scale(0, 2, 0, "S")
        z_square(0, 1, 1)
        m_mult(1, 1, 2)
        q_gate(1, 0, 1)
        m_copy(1, 1, 3, "S")
        z_mult(0, 1, 0)
        m_copy(1, 1, 2, "S")
        q_quant(1, 1, 1)
        q_turn(1, 3)
        q_quant(1, 0, 1)
        z_square(0, 1, 0)
        m_quant(1, 1)
        z_rsqrt(0, 1, 1)
        z_mult(0, 2, 1)
        q_quant(1, 0, 0)
        z_scale(0, 1, 1, "S")
        q_gate(1, 3, 0)
        z_mult(1, 0, 1)
        z_rsqrt(0, 1, 0)
        z_square(0, 2, 1)
        z_mult(1, 1, 1)
        z_scale(0, 1, 0, "V")
        z_square(1, 0, 1)
        q_gate(1, 3, 1)
        q_turn(1, 2)
        z_rsqrt(0, 2, 1)
        z_square(1, 1, 1)
        q_quant(1, 1, 0)
        z_rsqrt(1, 0, 1)
        z_scale(0, 2, 1, "S")
        z_mult(1, 0, 0)
        q_quant(1, 3, 1)
        q_gate(1, 2, 0)
        z_scale(1, 0, 1, "S")
        z_mult(1, 3, 1)
        z_rsqrt(1, 1, 1)
        z_square(1, 0, 0)
        z_mult(1, 1, 0)
        q_quant(1, 3, 0)
        z_scale(1, 1, 1, "S")
        q_gate(1, 2, 1)
        z_rsqrt(1, 0, 0)
        z_square(1, 3, 1)
        z_mult(1, 3, 0)
        z_scale(1, 0, 0, "S")
        q_quant(1, 2, 0)
        q_quant(1, 2, 1)
        z_rsqrt(1, 3, 1)
        z_square(1, 3, 0)
        z_mult(1, 2, 0)
        z_scale(1, 3, 1, "V")
        z_square(1, 1, 0)
        z_mult(1, 2, 1)
        z_rsqrt(1, 3, 0)
        z_square(1, 2, 0)
        z_scale(1, 3, 0, "V")
        z_rsqrt(1, 1, 0)
        z_square(1, 2, 1)
        z_scale(1, 1, 0, "V")
        z_rsqrt(1, 2, 0)
        z_rsqrt(1, 2, 1)
        z_scale(1, 2, 0, "S")
        z_scale(1, 2, 1, "V")
